import numpy as np
import ml_dtypes


def mxq(x, axis, fmt="e4m3"):
    dtype, down = {"e4m3": (ml_dtypes.float8_e4m3fn, 7), "e5m2": (ml_dtypes.float8_e5m2, 14)}[fmt]
    v = np.moveaxis(np.asarray(x, np.float32).astype(ml_dtypes.bfloat16).astype(np.float64), axis, -1)
    blocks = v.reshape(v.shape[:-1] + (-1, 32))
    amax = np.abs(blocks).max(-1, keepdims=True)
    byte = np.maximum(np.where(amax > 0, np.frexp(amax)[1] - 1 + 127, 0) - down, 1)
    scale = np.exp2(byte - 127.0)
    codes = (blocks / scale).astype(np.float32).astype(dtype).astype(np.float64)
    return np.moveaxis((codes * scale).reshape(v.shape), -1, axis)


WIDE = False


def mx_kscale(k):
    if not WIDE:
        return np.ones(k)
    levels = np.array([10, -10, 5, -5, 0])
    if k % 512:
        return np.exp2(np.random.permutation(np.resize(levels, k // 32))).repeat(32)
    a = np.empty((k // 512, 16))
    for p in range(k // 512):
        a[p, :8] = np.random.permutation(np.resize(levels, 8))
        for g in range(8):
            far = levels[np.abs(levels - a[p, g]) >= 10]
            a[p, g + 8] = far[np.random.randint(len(far))]
    return np.exp2(a.ravel()).repeat(32)


def f64(x):
    return np.asarray(x).astype(np.float64)


def striped(idx):
    return np.tile(idx.reshape(-1, 16).T, (8, 1)).astype(np.uint16)


def unstriped(offs):
    return offs[:16].T.reshape(-1).astype(np.int64)


E2M1 = np.array([0.0, 0.5, 1.0, 1.5, 2.0, 3.0, 4.0, 6.0, -0.0, -0.5, -1.0, -1.5, -2.0, -3.0, -4.0, -6.0])


def pack_weight(w, fmt):
    k, n = w.shape
    w = f64(np.asarray(w, np.float32).astype(ml_dtypes.bfloat16)).reshape(k // 32, 32, n)
    amax = np.abs(w).max(1)
    if fmt == "e4m3":
        byte = np.frexp(amax)[1] - 1 + 127 - 7
    else:
        mant, ex = np.frexp(amax / 6.0)
        byte = np.where(mant > 0.5, ex, ex - 1) + 127
    byte = np.clip(np.where(amax > 0, byte, 1), 1, 254)
    scaled = (w * np.exp2(127.0 - byte)[:, None, :]).reshape(k, n).astype(np.float32)
    by_word = np.ascontiguousarray(scaled.reshape(k // 512, 128, 4, n).transpose(0, 1, 3, 2))
    if fmt == "e4m3":
        words = by_word.astype(ml_dtypes.float8_e4m3fn).view(np.uint8)
    else:
        c = by_word.astype(ml_dtypes.float4_e2m1fn).view(np.uint8) & 0xF
        words = (c[..., 0::2] | (c[..., 1::2] << 4)).reshape(k // 512, 128, 2 * n)
    return np.ascontiguousarray(words), np.ascontiguousarray(byte.astype(np.uint8).reshape(k // 512, 16, n))


def unpack_weight(words, scales, fmt):
    g, _, n = scales.shape
    words = np.ascontiguousarray(words).reshape(g, 128, n, -1)
    if fmt == "e4m3":
        vals = words.view(ml_dtypes.float8_e4m3fn).astype(np.float64)
    else:
        nib = np.empty((g, 128, n, 4), np.uint8)
        nib[..., 0::2] = words & 0xF
        nib[..., 1::2] = words >> 4
        vals = E2M1[nib]
    vals = vals * np.repeat(np.exp2(scales.astype(np.float64) - 127.0), 8, axis=1)[..., None]
    return vals.transpose(0, 1, 3, 2).reshape(g * 512, n)


def gelu(v):
    return 0.5 * v * (1.0 + np.tanh(np.sqrt(2.0 / np.pi) * (v + 0.044715 * v**3)))


def bf(x):
    return np.asarray(x, np.float32).astype(ml_dtypes.bfloat16)


def planes(Y):
    n, m = Y.shape
    b = f64(bf(Y)).reshape(n // 32, 32, m)
    amax = np.abs(b).max(1)
    byte = np.clip(np.where(amax > 0, np.frexp(amax)[1] - 1 + 127 - 7, 1), 1, 254)
    codes = (b * np.exp2(127.0 - byte)[:, None, :]).reshape(n, m).astype(np.float32).astype(ml_dtypes.float8_e4m3fn).view(np.uint8)
    words = codes.reshape(n // 512, 128, 4, m).transpose(0, 1, 3, 2)
    return np.ascontiguousarray(words), np.ascontiguousarray(byte.astype(np.uint8).reshape(n // 512, 16, m))


K, T, S, H, N = 1024, 4096, 1024, 512, 768

def setup_inputs():
    n = np.random.standard_normal
    s = mx_kscale(K)[:, None]
    u = mx_kscale(H)[:, None]
    tab_words, tab_scales = pack_weight(n((K, T)) * s, "e4m3")
    w2_words, w2_scales = pack_weight(n((K, H)) / np.sqrt(K) / s * u.T, "e2m1")
    w4_words, w4_scales = pack_weight(n((H, N)) * 1.5 / np.sqrt(H) / u, "e4m3")
    return {
        "tab_words": tab_words, "tab_scales": tab_scales,
        "offs": striped(np.random.permutation(T)[:S]),
        "w1": (n((K, H)) * 1.5 / np.sqrt(K) / s).astype(np.float32),
        "w2_words": w2_words, "w2_scales": w2_scales,
        "w3": (n((K, H)) / np.sqrt(K) / s * u.T).astype(np.float32),
        "w4_words": w4_words, "w4_scales": w4_scales,
        "inv": np.abs(n((N, S))).astype(np.float32),
    }

def reference(tab_words, tab_scales, offs, w1, w2_words, w2_scales, w3, w4_words, w4_scales, inv):
    v = unpack_weight(tab_words, tab_scales, "e4m3")[:, unstriped(offs)]
    a = mxq(f64(w1), 0, "e4m3").T @ v
    gate = 1.0 / (1.0 + np.exp(-a))
    b = unpack_weight(w2_words, w2_scales, "e2m1").T @ v
    c = mxq(f64(w3), 0, "e4m3").T @ v
    h = c + gate * (b - c)
    words, scales = planes(h)
    d = unpack_weight(w4_words, w4_scales, "e4m3").T @ mxq(h, 0, "e4m3")
    y = d / (1.0 + f64(inv))
    return y, h, words, scales

@@ -1,0 +1,304 @@
+from contextlib import ExitStack
+
+import concourse.mybir as mybir
+
+K, T, S, H, N = 1024, 4096, 1024, 512, 768
+FLOPS = 2 * S * (3 * K * H + H * N)
+
+F32 = mybir.dt.float32
+BF16 = mybir.dt.bfloat16
+I32 = mybir.dt.int32
+U32 = mybir.dt.uint32
+U16 = mybir.dt.uint16
+U8 = mybir.dt.uint8
+FP8X4 = mybir.dt.float8_e4m3fn_x4
+FP4X4 = mybir.dt.float4_e2m1fn_x4
+ACT = mybir.ActivationFunctionType
+ALU = mybir.AluOpType
+
+P = 128
+PACK = 4
+K_PASS = P * PACK
+PASSES = K // K_PASS
+QUADS = 4
+HALF = 512
+HALVES = S // HALF
+N_TILES = N // P
+
+
+def tile_list_quote_smoothing_kernel(
+    tc, tab_words, tab_scales, offs, w1, w2_words, w2_scales, w3, w4_words, w4_scales, inv,
+    out_0, out_1, out_2, out_3,
+):
+    nc = tc.nc
+    with ExitStack() as ctx:
+        lists = ctx.enter_context(tc.tile_pool(name="lists", bufs=1))
+        keep = ctx.enter_context(tc.tile_pool(name="keep", bufs=1))
+        psum = ctx.enter_context(tc.psum_pool(name="psum", bufs=8))
+
+        def sb(name, shape, dtype):
+            return keep.tile(shape, dtype, name=name, align_bytes=64)
+
+        offsets = lists.tile([P, S // 16], U16, name="offsets")
+        tab_rows = sb("tab_rows", [P, T], U8)
+        w2_rows = sb("w2_rows", [P, PASSES * H], U8)
+        w4_plane = sb("w4_plane", [P, N], U8)
+        v_plane = [sb("v_plane%d" % a, [P, S], U8) for a in range(PASSES)]
+        one = sb("one", [P, 1], F32)
+        warm = sb("warm", [P, 1], F32)
+
+        nc.vector.memset(w2_rows[:].bitcast(I32), 0)
+        nc.vector.memset(one[:], 1.0)
+        nc.vector.memset(tab_rows[32:64, :].bitcast(I32), 0)
+        nc.vector.memset(tab_rows[64:128, :].bitcast(I32), 0)
+        for a in range(PASSES):
+            nc.vector.memset(v_plane[a][:].bitcast(I32), 0)
+        nc.vector.memset(w4_plane[:].bitcast(I32), 0)
+        nc.scalar.activation(warm[:], one[:], ACT.Sigmoid)
+
+        nc.sync.dma_start(offsets[:], offs)
+        nc.sync.dma_start(
+            tab_rows[0:32, :].bitcast(I32), tab_scales.rearrange("a q t -> (a q) t").bitcast(I32)
+        )
+        for q in range(QUADS):
+            nc.scalar.dma_start(
+                w2_rows[32 * q : 32 * q + 4, :].bitcast(I32).rearrange("r (a e) -> r a e", a=PASSES),
+                w2_scales[:, 4 * q : 4 * q + 4, :].bitcast(I32).rearrange("a r e -> r a e"),
+            )
+
+        def load_weight(name, w):
+            raws = []
+            for a in range(PASSES):
+                raw = sb("%s_raw%d" % (name, a), [P, PACK, H], F32)
+                nc.sync.dma_start(
+                    raw[:], w[a * K_PASS : (a + 1) * K_PASS, :].rearrange("(p j) c -> p j c", j=PACK)
+                )
+                raws.append(raw)
+            return raws
+
+        w1_raw = load_weight("w1", w1)
+        w2_raw = sb("w2_raw", [P, PASSES * 2 * H], U8)
+        nc.sync.dma_start(
+            w2_raw[:].bitcast(I32).rearrange("p (a e) -> p a e", a=PASSES),
+            w2_words.bitcast(I32).rearrange("a p e -> p a e"),
+        )
+        table = []
+        for a in range(PASSES):
+            tile = sb("table%d" % a, [P, T], I32)
+            nc.sync.dma_start(tile[:], tab_words[a].rearrange("p n i -> p (n i)").bitcast(I32))
+            table.append(tile)
+        w3_raw = load_weight("w3", w3)
+        w4_codes = sb("w4_codes", [P, N], I32)
+        nc.sync.dma_start(w4_codes[:], w4_words[0].rearrange("p n i -> p (n i)").bitcast(I32))
+        inv_view = inv.rearrange("(q p) j -> p q j", p=P)
+        PAIRS = N_TILES // 2
+        damp = {}
+        for h in range(HALVES):
+            for g in range(PAIRS):
+                tile = sb("inv%d_%d" % (h, g), [P, 2, HALF], F32)
+                nc.sync.dma_start(tile[:], inv_view[:, 2 * g : 2 * g + 2, h * HALF : (h + 1) * HALF])
+                damp[h, g] = tile
+
+        picked_rows = sb("picked_rows", [P, S], U8)
+        nc.vector.tensor_copy(picked_rows[:], tab_rows[:].indirect(offsets[:]))
+        for a in range(PASSES):
+            for q in range(QUADS):
+                row = 16 * a + 4 * q
+                nc.scalar.dma_start(
+                    v_plane[a][32 * q : 32 * q + 4, :].bitcast(I32),
+                    picked_rows[row : row + 4, :].bitcast(I32),
+                )
+        for q in range(QUADS):
+            nc.gpsimd.dma_start(
+                w4_plane[32 * q : 32 * q + 4, :].bitcast(I32),
+                w4_scales[0, 4 * q : 4 * q + 4, :].bitcast(I32),
+            )
+
+        def cast_scalar(out, in_):
+            nc.scalar.activation(out, in_, ACT.Copy)
+
+        def cast_gpsimd(out, in_):
+            nc.gpsimd.tensor_scalar(out, in_, 1.0, 0.0, ALU.mult, ALU.add)
+
+        def cast_vector(out, in_):
+            nc.vector.tensor_copy(out, in_)
+
+        def round_weight(name, raw, cast):
+            grouped = sb(name, [P, PACK * H], BF16)
+            cast(
+                grouped[:].rearrange("p (t m j) -> p m j t", t=PACK, j=PACK),
+                raw[:].rearrange("p j (m t) -> p m j t", t=PACK),
+            )
+            return grouped
+
+        def quantize_weight(name, grouped):
+            codes = sb(name + "_codes", [P, H], U32)
+            plane = sb(name + "_plane", [P, H], U8)
+            nc.vector.quantize_mx(out=codes[:].bitcast(FP8X4), scales=plane[:], in_=grouped[:])
+            return codes, plane
+
+        w1_bf = [round_weight("w1_bf%d" % a, w1_raw[a], cast_scalar) for a in range(PASSES)]
+
+        w2_codes = sb("w2_codes", [P, PASSES * 2 * H], U8)
+        nc.vector.tensor_copy(
+            w2_codes[:].rearrange("p (a t m b) -> p a m t b", a=PASSES, t=PACK, b=2),
+            w2_raw[:].rearrange("p (a m t b) -> p a m t b", a=PASSES, t=PACK, b=2),
+        )
+        w2_plane = sb("w2_plane", [P, PASSES * H], U8)
+        nc.vector.tensor_copy(
+            w2_plane[:].rearrange("p (a t m) -> p a m t", a=PASSES, t=PACK),
+            w2_rows[:].rearrange("p (a m t) -> p a m t", a=PASSES, t=PACK),
+        )
+        w1_mx = [quantize_weight("w1_%d" % a, w1_bf[a]) for a in range(PASSES)]
+
+        v_codes = {}
+
+        def gather(a, h):
+            tile = sb("v_codes%d_%d" % (a, h), [P, HALF], U32)
+            cols = HALF // 16
+            nc.vector.tensor_copy(
+                tile[:], table[a][:].bitcast(U32).indirect(offsets[:, h * cols : (h + 1) * cols])
+            )
+            v_codes[a, h] = tile
+
+        def fp8_operand(mx):
+            def pick(a, t):
+                codes, plane = mx[a]
+                return codes[:, t * P : (t + 1) * P].bitcast(FP8X4), plane[:, t * P : (t + 1) * P]
+            return pick
+
+        def w2_operand(a, t):
+            col = a * H + t * P
+            return w2_codes[:, 2 * col : 2 * (col + P)].bitcast(FP4X4), w2_plane[:, col : col + P]
+
+        def bank(name):
+            return psum.tile([P, HALF], F32, name=name, tag="bank")
+
+        def mx_pass(acc, operand, a, t, h):
+            codes, plane = operand(a, t)
+            nc.tensor.matmul_mx(
+                out=acc[:], lhsT=codes, lhsT_scale=plane,
+                rhs=v_codes[a, h][:].bitcast(FP8X4),
+                rhs_scale=v_plane[a][:, h * HALF : (h + 1) * HALF],
+                start=(a == 0), stop=(a == PASSES - 1),
+            )
+
+        w1_operand = fp8_operand(w1_mx)
+        gate = [[sb("gate%d_%d" % (h, t), [P, HALF], F32) for t in range(PACK)] for h in range(HALVES)]
+        fresh = [sb("fresh%d" % h, [P, PACK, HALF], F32) for h in range(HALVES)]
+        slow = [sb("slow%d" % h, [P, PACK, HALF], F32) for h in range(HALVES)]
+        smooth = [sb("smooth%d" % h, [P, PACK, HALF], F32) for h in range(HALVES)]
+
+        gather(0, 0)
+        gather(0, 1)
+        acc_a = [bank("a0_%d" % t) for t in range(PACK)]
+        acc_b = [bank("b0_%d" % t) for t in range(PACK)]
+        for t in range(PACK):
+            mx_pass(acc_a[t], w1_operand, 0, t, 0)
+            mx_pass(acc_b[t], w2_operand, 0, t, 0)
+        gather(1, 0)
+        gather(1, 1)
+        for t in range(PACK):
+            mx_pass(acc_a[t], w1_operand, 1, t, 0)
+            mx_pass(acc_b[t], w2_operand, 1, t, 0)
+        for t in range(PACK):
+            nc.scalar.activation(gate[0][t][:], acc_a[t][:], ACT.Sigmoid)
+            nc.vector.tensor_tensor(fresh[0][:, t, :], acc_b[t][:], gate[0][t][:], ALU.mult)
+
+        w3_bf = [round_weight("w3_bf0", w3_raw[0], cast_vector)]
+
+        for t in range(PACK):
+            acc_a = bank("a1_%d" % t)
+            acc_b = bank("b1_%d" % t)
+            for a in range(PASSES):
+                mx_pass(acc_a, w1_operand, a, t, 1)
+            for a in range(PASSES):
+                mx_pass(acc_b, w2_operand, a, t, 1)
+            nc.scalar.activation(gate[1][t][:], acc_a[:], ACT.Sigmoid)
+            nc.vector.tensor_tensor(fresh[1][:, t, :], acc_b[:], gate[1][t][:], ALU.mult)
+            if t == 0:
+                w3_mx = [quantize_weight("w3_0", w3_bf[0])]
+        codes = sb("w3_1_codes", [P, H], U32)
+        plane = sb("w3_1_plane", [P, H], U8)
+        for u, cast in enumerate((cast_vector, cast_scalar)):
+            grouped = sb("w3_bf1_%d" % u, [P, 2 * H], BF16)
+            cast(
+                grouped[:].rearrange("p (t m j) -> p m j t", t=2, j=PACK),
+                w3_raw[1][:].rearrange("p j (m t) -> p m j t", t=PACK)[:, :, :, 2 * u : 2 * u + 2],
+            )
+            cols = slice(2 * u * P, 2 * (u + 1) * P)
+            nc.vector.quantize_mx(out=codes[:, cols].bitcast(FP8X4), scales=plane[:, cols], in_=grouped[:])
+        w3_mx.append((codes, plane))
+        w3_operand = fp8_operand(w3_mx)
+
+        def damping(h):
+            for g in range(PAIRS):
+                flat = damp[h, g][:].rearrange("p q j -> p (q j)")
+                nc.scalar.activation(flat, flat, ACT.Abs_reciprocal_sqrt, bias=one[:])
+                nc.scalar.activation(flat, flat, ACT.Square)
+
+        h_codes = sb("h_codes", [P, S], U32)
+        h_plane = sb("h_plane", [P, S], U8)
+        h_view = out_1.rearrange("(p t) j -> p t j", t=PACK)
+        words_view = out_2[0].rearrange("p m i -> p (m i)").bitcast(I32)
+        y_view = out_0.rearrange("(q p) j -> p q j", p=P)
+
+        def smooth_half(h):
+            for t in range(PACK):
+                acc_c = bank("c%d_%d" % (h, t))
+                for a in range(PASSES):
+                    mx_pass(acc_c, w3_operand, a, t, h)
+                nc.vector.scalar_tensor_tensor(
+                    slow[h][:, t, :], gate[h][t][:], 1.0, acc_c[:], ALU.subtract, ALU.mult
+                )
+            for t in range(0, PACK, 2):
+                pair = slice(t, t + 2)
+                nc.vector.tensor_tensor(smooth[h][:, pair, :], fresh[h][:, pair, :], slow[h][:, pair, :], ALU.subtract)
+                nc.sync.dma_start(h_view[:, pair, h * HALF : (h + 1) * HALF], smooth[h][:, pair, :])
+
+        woven_tiles = {}
+
+        def weave_half(h):
+            woven = sb("woven%d" % h, [P, PACK * HALF], BF16)
+            cast_scalar(
+                woven[:].rearrange("p (c i t) -> p c t i", i=4, t=PACK),
+                smooth[h][:].rearrange("p t (c i) -> p c t i", i=4),
+            )
+            woven_tiles[h] = woven
+
+        def quantize_half(h):
+            cols = slice(h * HALF, (h + 1) * HALF)
+            woven = woven_tiles[h]
+            nc.vector.quantize_mx(out=h_codes[:, cols].bitcast(FP8X4), scales=h_plane[:, cols], in_=woven[:])
+            nc.sync.dma_start(words_view[:, cols], h_codes[:, cols].bitcast(I32))
+
+        def adjust_half(h):
+            cols = slice(h * HALF, (h + 1) * HALF)
+            for g in range(PAIRS):
+                y = damp[h, g]
+                for i in range(2):
+                    n0 = (2 * g + i) * P
+                    acc_d = bank("d%d_%d_%d" % (h, g, i))
+                    nc.tensor.matmul_mx(
+                        out=acc_d[:], lhsT=w4_codes[:, n0 : n0 + P].bitcast(FP8X4),
+                        lhsT_scale=w4_plane[:, n0 : n0 + P],
+                        rhs=h_codes[:, cols].bitcast(FP8X4), rhs_scale=h_plane[:, cols],
+                        start=True, stop=True,
+                    )
+                    nc.vector.tensor_tensor(y[:, i, :], acc_d[:], damp[h, g][:, i, :], ALU.mult)
+                nc.sync.dma_start(y_view[:, 2 * g : 2 * g + 2, cols], y[:])
+
+        damping(0)
+        smooth_half(0)
+        weave_half(0)
+        quantize_half(0)
+        smooth_half(1)
+        weave_half(1)
+        quantize_half(1)
+        damping(1)
+        adjust_half(0)
+        for q in range(QUADS):
+            nc.scalar.dma_start(
+                out_3[0, 4 * q : 4 * q + 4, :].bitcast(I32), h_plane[32 * q : 32 * q + 4, :].bitcast(I32)
+            )
+        adjust_half(1)

@@ -34,7 +34,7 @@ def tile_list_quote_smoothing_kernel(
     with ExitStack() as ctx:
         lists = ctx.enter_context(tc.tile_pool(name="lists", bufs=1))
         keep = ctx.enter_context(tc.tile_pool(name="keep", bufs=1))
-        psum = ctx.enter_context(tc.psum_pool(name="psum", bufs=8))
+        psum = ctx.enter_context(tc.psum_pool(name="psum", bufs=1))
 
         def sb(name, shape, dtype):
             return keep.tile(shape, dtype, name=name, align_bytes=64)
@@ -49,7 +49,7 @@ def tile_list_quote_smoothing_kernel(
 
         nc.vector.memset(w2_rows[:].bitcast(I32), 0)
         nc.vector.memset(one[:], 1.0)
-        nc.vector.memset(tab_rows[32:64, :].bitcast(I32), 0)
+        nc.gpsimd.memset(tab_rows[32:64, :].bitcast(I32), 0)
         nc.vector.memset(tab_rows[64:128, :].bitcast(I32), 0)
         for a in range(PASSES):
             nc.vector.memset(v_plane[a][:].bitcast(I32), 0)
@@ -76,17 +76,25 @@ def tile_list_quote_smoothing_kernel(
                 raws.append(raw)
             return raws
 
-        w1_raw = load_weight("w1", w1)
         w2_raw = sb("w2_raw", [P, PASSES * 2 * H], U8)
         nc.sync.dma_start(
             w2_raw[:].bitcast(I32).rearrange("p (a e) -> p a e", a=PASSES),
             w2_words.bitcast(I32).rearrange("a p e -> p a e"),
         )
+        w1_raw = load_weight("w1", w1)
+        picked_rows = sb("picked_rows", [P, S], U8)
+        nc.vector.tensor_copy(picked_rows[:], tab_rows[:].indirect(offsets[:]))
         table = []
         for a in range(PASSES):
             tile = sb("table%d" % a, [P, T], I32)
             nc.sync.dma_start(tile[:], tab_words[a].rearrange("p n i -> p (n i)").bitcast(I32))
             table.append(tile)
+            for q in range(QUADS):
+                row = 16 * a + 4 * q
+                nc.sync.dma_start(
+                    v_plane[a][32 * q : 32 * q + 4, :].bitcast(I32),
+                    picked_rows[row : row + 4, :].bitcast(I32),
+                )
         w3_raw = load_weight("w3", w3)
         w4_codes = sb("w4_codes", [P, N], I32)
         nc.sync.dma_start(w4_codes[:], w4_words[0].rearrange("p n i -> p (n i)").bitcast(I32))
@@ -99,15 +107,6 @@ def tile_list_quote_smoothing_kernel(
                 nc.sync.dma_start(tile[:], inv_view[:, 2 * g : 2 * g + 2, h * HALF : (h + 1) * HALF])
                 damp[h, g] = tile
 
-        picked_rows = sb("picked_rows", [P, S], U8)
-        nc.vector.tensor_copy(picked_rows[:], tab_rows[:].indirect(offsets[:]))
-        for a in range(PASSES):
-            for q in range(QUADS):
-                row = 16 * a + 4 * q
-                nc.scalar.dma_start(
-                    v_plane[a][32 * q : 32 * q + 4, :].bitcast(I32),
-                    picked_rows[row : row + 4, :].bitcast(I32),
-                )
         for q in range(QUADS):
             nc.gpsimd.dma_start(
                 w4_plane[32 * q : 32 * q + 4, :].bitcast(I32),
@@ -171,8 +170,8 @@ def tile_list_quote_smoothing_kernel(
             col = a * H + t * P
             return w2_codes[:, 2 * col : 2 * (col + P)].bitcast(FP4X4), w2_plane[:, col : col + P]
 
-        def bank(name):
-            return psum.tile([P, HALF], F32, name=name, tag="bank")
+        def bank(name, slot):
+            return psum.tile([P, HALF], F32, name=name, tag="bank%d" % slot)
 
         def mx_pass(acc, operand, a, t, h):
             codes, plane = operand(a, t)
@@ -189,10 +188,85 @@ def tile_list_quote_smoothing_kernel(
         slow = [sb("slow%d" % h, [P, PACK, HALF], F32) for h in range(HALVES)]
         smooth = [sb("smooth%d" % h, [P, PACK, HALF], F32) for h in range(HALVES)]
 
+        h_codes = sb("h_codes", [P, S], U32)
+        h_plane = sb("h_plane", [P, S], U8)
+        h_view = out_1.rearrange("(p t) j -> p t j", t=PACK)
+        words_view = out_2[0].rearrange("p m i -> p (m i)").bitcast(I32)
+        y_view = out_0.rearrange("(q p) j -> p q j", p=P)
+        woven = [sb("woven%d" % h, [P, PACK * HALF], BF16) for h in range(HALVES)]
+
+        def gate_of(h, t, acc):
+            nc.scalar.activation(gate[h][t][:], acc[:], ACT.Sigmoid)
+
+        def fresh_of(h, t, acc):
+            nc.vector.tensor_tensor(fresh[h][:, t, :], acc[:], gate[h][t][:], ALU.mult)
+
+        def slow_of(h, t):
+            acc = bank("c%d_%d" % (h, t), t)
+            for a in range(PASSES):
+                mx_pass(acc, w3_operand, a, t, h)
+            nc.vector.scalar_tensor_tensor(slow[h][:, t, :], gate[h][t][:], 1.0, acc[:], ALU.subtract, ALU.mult)
+
+        def smooth_pair(h, u, on_vector):
+            pair = slice(2 * u, 2 * u + 2)
+            if on_vector:
+                nc.vector.tensor_tensor(smooth[h][:, pair, :], fresh[h][:, pair, :], slow[h][:, pair, :], ALU.subtract)
+            else:
+                for t in range(2 * u, 2 * u + 2):
+                    nc.gpsimd.tensor_tensor(smooth[h][:, t, :], fresh[h][:, t, :], slow[h][:, t, :], ALU.subtract)
+            nc.sync.dma_start(h_view[:, pair, h * HALF : (h + 1) * HALF], smooth[h][:, pair, :])
+
+        def weave(h):
+            cast_scalar(
+                woven[h][:].rearrange("p (c i t) -> p c t i", i=4, t=PACK),
+                smooth[h][:].rearrange("p t (c i) -> p c t i", i=4),
+            )
+
+        def quantize_half(h):
+            cols = slice(h * HALF, (h + 1) * HALF)
+            nc.vector.quantize_mx(out=h_codes[:, cols].bitcast(FP8X4), scales=h_plane[:, cols], in_=woven[h][:])
+            nc.sync.dma_start(words_view[:, cols], h_codes[:, cols].bitcast(I32))
+
+        def root(h, g):
+            flat = damp[h, g][:].rearrange("p q j -> p (q j)")
+            nc.scalar.activation(flat, flat, ACT.Abs_reciprocal_sqrt, bias=one[:])
+
+        def square_scalar(h, g):
+            flat = damp[h, g][:].rearrange("p q j -> p (q j)")
+            nc.scalar.activation(flat, flat, ACT.Square)
+
+        def square_gpsimd(h, g):
+            for i in range(2):
+                part = damp[h, g][:, i, :]
+                nc.gpsimd.tensor_tensor(part, part, part, ALU.mult)
+
+        def damping(h, g):
+            root(h, g)
+            square_scalar(h, g)
+
+        def adjust(h, g, split=False):
+            cols = slice(h * HALF, (h + 1) * HALF)
+            y = damp[h, g]
+            for i in range(2):
+                q = 2 * g + i
+                n0 = q * P
+                acc = bank("d%d_%d" % (h, q), PACK + (h * N_TILES + q) % PACK)
+                nc.tensor.matmul_mx(
+                    out=acc[:], lhsT=w4_codes[:, n0 : n0 + P].bitcast(FP8X4),
+                    lhsT_scale=w4_plane[:, n0 : n0 + P],
+                    rhs=h_codes[:, cols].bitcast(FP8X4), rhs_scale=h_plane[:, cols],
+                    start=True, stop=True,
+                )
+                nc.vector.tensor_tensor(y[:, i, :], acc[:], y[:, i, :], ALU.mult)
+                if split:
+                    nc.sync.dma_start(y_view[:, q, cols], y[:, i, :])
+            if not split:
+                nc.sync.dma_start(y_view[:, 2 * g : 2 * g + 2, cols], y[:])
+
         gather(0, 0)
         gather(0, 1)
-        acc_a = [bank("a0_%d" % t) for t in range(PACK)]
-        acc_b = [bank("b0_%d" % t) for t in range(PACK)]
+        acc_a = [bank("a0_%d" % t, t) for t in range(PACK)]
+        acc_b = [bank("b0_%d" % t, PACK + t) for t in range(PACK)]
         for t in range(PACK):
             mx_pass(acc_a[t], w1_operand, 0, t, 0)
             mx_pass(acc_b[t], w2_operand, 0, t, 0)
@@ -202,22 +276,19 @@ def tile_list_quote_smoothing_kernel(
             mx_pass(acc_a[t], w1_operand, 1, t, 0)
             mx_pass(acc_b[t], w2_operand, 1, t, 0)
         for t in range(PACK):
-            nc.scalar.activation(gate[0][t][:], acc_a[t][:], ACT.Sigmoid)
-            nc.vector.tensor_tensor(fresh[0][:, t, :], acc_b[t][:], gate[0][t][:], ALU.mult)
-
-        w3_bf = [round_weight("w3_bf0", w3_raw[0], cast_vector)]
-
+            gate_of(0, t, acc_a[t])
+            fresh_of(0, t, acc_b[t])
         for t in range(PACK):
-            acc_a = bank("a1_%d" % t)
-            acc_b = bank("b1_%d" % t)
+            acc = bank("a1_%d" % t, t)
             for a in range(PASSES):
-                mx_pass(acc_a, w1_operand, a, t, 1)
+                mx_pass(acc, w1_operand, a, t, 1)
+            gate_of(1, t, acc)
+        acc_b = [bank("b1_%d" % t, PACK + t) for t in range(PACK)]
+        for t in range(PACK):
             for a in range(PASSES):
-                mx_pass(acc_b, w2_operand, a, t, 1)
-            nc.scalar.activation(gate[1][t][:], acc_a[:], ACT.Sigmoid)
-            nc.vector.tensor_tensor(fresh[1][:, t, :], acc_b[:], gate[1][t][:], ALU.mult)
-            if t == 0:
-                w3_mx = [quantize_weight("w3_0", w3_bf[0])]
+                mx_pass(acc_b[t], w2_operand, a, t, 1)
+
+        w3_mx = [quantize_weight("w3_0", round_weight("w3_bf0", w3_raw[0], cast_vector))]
         codes = sb("w3_1_codes", [P, H], U32)
         plane = sb("w3_1_plane", [P, H], U8)
         for u, cast in enumerate((cast_vector, cast_scalar)):
@@ -231,74 +302,37 @@ def tile_list_quote_smoothing_kernel(
         w3_mx.append((codes, plane))
         w3_operand = fp8_operand(w3_mx)
 
-        def damping(h):
-            for g in range(PAIRS):
-                flat = damp[h, g][:].rearrange("p q j -> p (q j)")
-                nc.scalar.activation(flat, flat, ACT.Abs_reciprocal_sqrt, bias=one[:])
-                nc.scalar.activation(flat, flat, ACT.Square)
-
-        h_codes = sb("h_codes", [P, S], U32)
-        h_plane = sb("h_plane", [P, S], U8)
-        h_view = out_1.rearrange("(p t) j -> p t j", t=PACK)
-        words_view = out_2[0].rearrange("p m i -> p (m i)").bitcast(I32)
-        y_view = out_0.rearrange("(q p) j -> p q j", p=P)
-
-        def smooth_half(h):
-            for t in range(PACK):
-                acc_c = bank("c%d_%d" % (h, t))
-                for a in range(PASSES):
-                    mx_pass(acc_c, w3_operand, a, t, h)
-                nc.vector.scalar_tensor_tensor(
-                    slow[h][:, t, :], gate[h][t][:], 1.0, acc_c[:], ALU.subtract, ALU.mult
-                )
-            for t in range(0, PACK, 2):
-                pair = slice(t, t + 2)
-                nc.vector.tensor_tensor(smooth[h][:, pair, :], fresh[h][:, pair, :], slow[h][:, pair, :], ALU.subtract)
-                nc.sync.dma_start(h_view[:, pair, h * HALF : (h + 1) * HALF], smooth[h][:, pair, :])
-
-        woven_tiles = {}
-
-        def weave_half(h):
-            woven = sb("woven%d" % h, [P, PACK * HALF], BF16)
-            cast_scalar(
-                woven[:].rearrange("p (c i t) -> p c t i", i=4, t=PACK),
-                smooth[h][:].rearrange("p t (c i) -> p c t i", i=4),
-            )
-            woven_tiles[h] = woven
-
-        def quantize_half(h):
-            cols = slice(h * HALF, (h + 1) * HALF)
-            woven = woven_tiles[h]
-            nc.vector.quantize_mx(out=h_codes[:, cols].bitcast(FP8X4), scales=h_plane[:, cols], in_=woven[:])
-            nc.sync.dma_start(words_view[:, cols], h_codes[:, cols].bitcast(I32))
-
-        def adjust_half(h):
-            cols = slice(h * HALF, (h + 1) * HALF)
-            for g in range(PAIRS):
-                y = damp[h, g]
-                for i in range(2):
-                    n0 = (2 * g + i) * P
-                    acc_d = bank("d%d_%d_%d" % (h, g, i))
-                    nc.tensor.matmul_mx(
-                        out=acc_d[:], lhsT=w4_codes[:, n0 : n0 + P].bitcast(FP8X4),
-                        lhsT_scale=w4_plane[:, n0 : n0 + P],
-                        rhs=h_codes[:, cols].bitcast(FP8X4), rhs_scale=h_plane[:, cols],
-                        start=True, stop=True,
-                    )
-                    nc.vector.tensor_tensor(y[:, i, :], acc_d[:], damp[h, g][:, i, :], ALU.mult)
-                nc.sync.dma_start(y_view[:, 2 * g : 2 * g + 2, cols], y[:])
-
-        damping(0)
-        smooth_half(0)
-        weave_half(0)
+        fresh_of(1, 0, acc_b[0])
+        fresh_of(1, 1, acc_b[1])
+        damping(0, 0)
+        damping(0, 1)
+        root(0, 2)
+        for t in range(PACK):
+            slow_of(0, t)
+        smooth_pair(0, 0, False)
+        smooth_pair(0, 1, False)
+        weave(0)
+        fresh_of(1, 2, acc_b[2])
+        fresh_of(1, 3, acc_b[3])
+        root(1, 0)
+        for t in range(PACK):
+            slow_of(1, t)
+        smooth_pair(1, 0, False)
+        smooth_pair(1, 1, True)
         quantize_half(0)
-        smooth_half(1)
-        weave_half(1)
+        weave(1)
+        square_gpsimd(0, 2)
+        square_gpsimd(1, 0)
+        damping(1, 1)
+        damping(1, 2)
+        adjust(0, 0)
+        adjust(0, 1)
         quantize_half(1)
-        damping(1)
-        adjust_half(0)
         for q in range(QUADS):
-            nc.scalar.dma_start(
+            nc.sync.dma_start(
                 out_3[0, 4 * q : 4 * q + 4, :].bitcast(I32), h_plane[32 * q : 32 * q + 4, :].bitcast(I32)
             )
-        adjust_half(1)
+        adjust(0, 2)
+        adjust(1, 0)
+        adjust(1, 1)
+        adjust(1, 2, split=True)

@@ -101,11 +101,11 @@ def tile_list_quote_smoothing_kernel(
         inv_view = inv.rearrange("(q p) j -> p q j", p=P)
         PAIRS = N_TILES // 2
         damp = {}
-        for h in range(HALVES):
-            for g in range(PAIRS):
-                tile = sb("inv%d_%d" % (h, g), [P, 2, HALF], F32)
-                nc.sync.dma_start(tile[:], inv_view[:, 2 * g : 2 * g + 2, h * HALF : (h + 1) * HALF])
-                damp[h, g] = tile
+        for g in range(PAIRS):
+            tile = sb("inv%d" % g, [P, 2, S], F32)
+            nc.sync.dma_start(tile[:], inv_view[:, 2 * g : 2 * g + 2, :])
+            for h in range(HALVES):
+                damp[h, g] = tile[:, :, h * HALF : (h + 1) * HALF]
 
         for q in range(QUADS):
             nc.gpsimd.dma_start(
@@ -199,7 +199,7 @@ def tile_list_quote_smoothing_kernel(
             nc.scalar.activation(gate[h][t][:], acc[:], ACT.Sigmoid)
 
         def fresh_of(h, t, acc):
-            nc.vector.tensor_tensor(fresh[h][:, t, :], acc[:], gate[h][t][:], ALU.mult)
+            nc.vector.tensor_tensor(fresh[h][:, t, :], gate[h][t][:], acc[:], ALU.mult)
 
         def slow_of(h, t):
             acc = bank("c%d_%d" % (h, t), t)
@@ -228,11 +228,11 @@ def tile_list_quote_smoothing_kernel(
             nc.sync.dma_start(words_view[:, cols], h_codes[:, cols].bitcast(I32))
 
         def root(h, g):
-            flat = damp[h, g][:].rearrange("p q j -> p (q j)")
+            flat = damp[h, g]
             nc.scalar.activation(flat, flat, ACT.Abs_reciprocal_sqrt, bias=one[:])
 
         def square_scalar(h, g):
-            flat = damp[h, g][:].rearrange("p q j -> p (q j)")
+            flat = damp[h, g]
             nc.scalar.activation(flat, flat, ACT.Square)
 
         def square_gpsimd(h, g):
@@ -243,6 +243,12 @@ def tile_list_quote_smoothing_kernel(
         def damping(h, g):
             root(h, g)
             square_scalar(h, g)
+
+        def damping_by_tile(h, g):
+            for i in range(2):
+                part = damp[h, g][:, i, :]
+                nc.scalar.activation(part, part, ACT.Abs_reciprocal_sqrt, bias=one[:])
+                nc.scalar.activation(part, part, ACT.Square)
 
         def adjust(h, g, split=False):
             cols = slice(h * HALF, (h + 1) * HALF)
@@ -257,11 +263,11 @@ def tile_list_quote_smoothing_kernel(
                     rhs=h_codes[:, cols].bitcast(FP8X4), rhs_scale=h_plane[:, cols],
                     start=True, stop=True,
                 )
-                nc.vector.tensor_tensor(y[:, i, :], acc[:], y[:, i, :], ALU.mult)
+                nc.vector.tensor_tensor(y[:, i, :], y[:, i, :], acc[:], ALU.mult)
                 if split:
                     nc.sync.dma_start(y_view[:, q, cols], y[:, i, :])
             if not split:
-                nc.sync.dma_start(y_view[:, 2 * g : 2 * g + 2, cols], y[:])
+                nc.sync.dma_start(y_view[:, 2 * g : 2 * g + 2, cols], y)
 
         gather(0, 0)
         gather(0, 1)
@@ -303,7 +309,6 @@ def tile_list_quote_smoothing_kernel(
         w3_operand = fp8_operand(w3_mx)
 
         fresh_of(1, 0, acc_b[0])
-        fresh_of(1, 1, acc_b[1])
         damping(0, 0)
         damping(0, 1)
         root(0, 2)
@@ -312,19 +317,19 @@ def tile_list_quote_smoothing_kernel(
         smooth_pair(0, 0, False)
         smooth_pair(0, 1, False)
         weave(0)
-        fresh_of(1, 2, acc_b[2])
-        fresh_of(1, 3, acc_b[3])
-        root(1, 0)
+        for t in range(1, PACK):
+            fresh_of(1, t, acc_b[t])
         for t in range(PACK):
             slow_of(1, t)
-        smooth_pair(1, 0, False)
-        smooth_pair(1, 1, True)
+        smooth_pair(1, 0, True)
         quantize_half(0)
+        smooth_pair(1, 1, True)
         weave(1)
+        root(1, 0)
         square_gpsimd(0, 2)
         square_gpsimd(1, 0)
         damping(1, 1)
-        damping(1, 2)
+        damping_by_tile(1, 2)
         adjust(0, 0)
         adjust(0, 1)
         quantize_half(1)

@@ -49,7 +49,7 @@ def tile_list_quote_smoothing_kernel(
 
         nc.vector.memset(w2_rows[:].bitcast(I32), 0)
         nc.vector.memset(one[:], 1.0)
-        nc.gpsimd.memset(tab_rows[32:64, :].bitcast(I32), 0)
+        nc.vector.memset(tab_rows[32:64, :].bitcast(I32), 0)
         nc.vector.memset(tab_rows[64:128, :].bitcast(I32), 0)
         for a in range(PASSES):
             nc.vector.memset(v_plane[a][:].bitcast(I32), 0)
@@ -98,20 +98,19 @@ def tile_list_quote_smoothing_kernel(
         w3_raw = load_weight("w3", w3)
         w4_codes = sb("w4_codes", [P, N], I32)
         nc.sync.dma_start(w4_codes[:], w4_words[0].rearrange("p n i -> p (n i)").bitcast(I32))
-        inv_view = inv.rearrange("(q p) j -> p q j", p=P)
-        PAIRS = N_TILES // 2
-        damp = {}
-        for g in range(PAIRS):
-            tile = sb("inv%d" % g, [P, 2, S], F32)
-            nc.sync.dma_start(tile[:], inv_view[:, 2 * g : 2 * g + 2, :])
-            for h in range(HALVES):
-                damp[h, g] = tile[:, :, h * HALF : (h + 1) * HALF]
-
         for q in range(QUADS):
-            nc.gpsimd.dma_start(
+            nc.sync.dma_start(
                 w4_plane[32 * q : 32 * q + 4, :].bitcast(I32),
                 w4_scales[0, 4 * q : 4 * q + 4, :].bitcast(I32),
             )
+        inv_view = inv.rearrange("(q p) j -> p q j", p=P)
+        PAIRS = N_TILES // 2
+        damp = {}
+        for h in range(HALVES):
+            for g in range(PAIRS):
+                tile = sb("inv%d_%d" % (h, g), [P, 2, HALF], F32)
+                nc.sync.dma_start(tile[:], inv_view[:, 2 * g : 2 * g + 2, h * HALF : (h + 1) * HALF])
+                damp[h, g] = tile[:]
 
         def cast_scalar(out, in_):
             nc.scalar.activation(out, in_, ACT.Copy)
@@ -122,11 +121,11 @@ def tile_list_quote_smoothing_kernel(
         def cast_vector(out, in_):
             nc.vector.tensor_copy(out, in_)
 
-        def round_weight(name, raw, cast):
+        def round_weight(name, raw, cast, walk):
             grouped = sb(name, [P, PACK * H], BF16)
             cast(
-                grouped[:].rearrange("p (t m j) -> p m j t", t=PACK, j=PACK),
-                raw[:].rearrange("p j (m t) -> p m j t", t=PACK),
+                grouped[:].rearrange("p (t m j) -> p " + walk, t=PACK, j=PACK),
+                raw[:].rearrange("p j (m t) -> p " + walk, t=PACK),
             )
             return grouped
 
@@ -136,17 +135,17 @@ def tile_list_quote_smoothing_kernel(
             nc.vector.quantize_mx(out=codes[:].bitcast(FP8X4), scales=plane[:], in_=grouped[:])
             return codes, plane
 
-        w1_bf = [round_weight("w1_bf%d" % a, w1_raw[a], cast_scalar) for a in range(PASSES)]
+        w1_bf = [round_weight("w1_bf%d" % a, w1_raw[a], cast_scalar, "m j t") for a in range(PASSES)]
 
         w2_codes = sb("w2_codes", [P, PASSES * 2 * H], U8)
         nc.vector.tensor_copy(
-            w2_codes[:].rearrange("p (a t m b) -> p a m t b", a=PASSES, t=PACK, b=2),
-            w2_raw[:].rearrange("p (a m t b) -> p a m t b", a=PASSES, t=PACK, b=2),
+            w2_codes[:].rearrange("p (a t m b) -> p a t m b", a=PASSES, t=PACK, b=2),
+            w2_raw[:].rearrange("p (a m t b) -> p a t m b", a=PASSES, t=PACK, b=2),
         )
         w2_plane = sb("w2_plane", [P, PASSES * H], U8)
         nc.vector.tensor_copy(
-            w2_plane[:].rearrange("p (a t m) -> p a m t", a=PASSES, t=PACK),
-            w2_rows[:].rearrange("p (a m t) -> p a m t", a=PASSES, t=PACK),
+            w2_plane[:].rearrange("p (a t m) -> p a t m", a=PASSES, t=PACK),
+            w2_rows[:].rearrange("p (a m t) -> p a t m", a=PASSES, t=PACK),
         )
         w1_mx = [quantize_weight("w1_%d" % a, w1_bf[a]) for a in range(PASSES)]
 
@@ -294,40 +293,45 @@ def tile_list_quote_smoothing_kernel(
             for a in range(PASSES):
                 mx_pass(acc_b[t], w2_operand, a, t, 1)
 
-        w3_mx = [quantize_weight("w3_0", round_weight("w3_bf0", w3_raw[0], cast_vector))]
+        w3_bf0 = round_weight("w3_bf0", w3_raw[0], cast_vector, "m j t")
+        fresh_of(1, 0, acc_b[0])
+        w3_mx = [quantize_weight("w3_0", w3_bf0)]
         codes = sb("w3_1_codes", [P, H], U32)
         plane = sb("w3_1_plane", [P, H], U8)
+        w3_bf1 = []
         for u, cast in enumerate((cast_vector, cast_scalar)):
             grouped = sb("w3_bf1_%d" % u, [P, 2 * H], BF16)
             cast(
                 grouped[:].rearrange("p (t m j) -> p m j t", t=2, j=PACK),
                 w3_raw[1][:].rearrange("p j (m t) -> p m j t", t=PACK)[:, :, :, 2 * u : 2 * u + 2],
             )
+            w3_bf1.append(grouped)
+        fresh_of(1, 1, acc_b[1])
+        for u in range(2):
             cols = slice(2 * u * P, 2 * (u + 1) * P)
-            nc.vector.quantize_mx(out=codes[:, cols].bitcast(FP8X4), scales=plane[:, cols], in_=grouped[:])
+            nc.vector.quantize_mx(out=codes[:, cols].bitcast(FP8X4), scales=plane[:, cols], in_=w3_bf1[u][:])
         w3_mx.append((codes, plane))
         w3_operand = fp8_operand(w3_mx)
 
-        fresh_of(1, 0, acc_b[0])
+        fresh_of(1, 2, acc_b[2])
         damping(0, 0)
         damping(0, 1)
         root(0, 2)
         for t in range(PACK):
             slow_of(0, t)
-        smooth_pair(0, 0, False)
-        smooth_pair(0, 1, False)
+        smooth_pair(0, 0, True)
+        smooth_pair(0, 1, True)
         weave(0)
-        for t in range(1, PACK):
-            fresh_of(1, t, acc_b[t])
-        for t in range(PACK):
+        square_scalar(0, 2)
+        fresh_of(1, 3, acc_b[3])
+        for t in range(PACK - 1):
             slow_of(1, t)
-        smooth_pair(1, 0, True)
         quantize_half(0)
+        slow_of(1, PACK - 1)
+        smooth_pair(1, 0, True)
         smooth_pair(1, 1, True)
         weave(1)
-        root(1, 0)
-        square_gpsimd(0, 2)
-        square_gpsimd(1, 0)
+        damping(1, 0)
         damping(1, 1)
         damping_by_tile(1, 2)
         adjust(0, 0)

@@ -45,7 +45,6 @@ def tile_list_quote_smoothing_kernel(
         w4_plane = sb("w4_plane", [P, N], U8)
         v_plane = [sb("v_plane%d" % a, [P, S], U8) for a in range(PASSES)]
         one = sb("one", [P, 1], F32)
-        warm = sb("warm", [P, 1], F32)
 
         nc.vector.memset(w2_rows[:].bitcast(I32), 0)
         nc.vector.memset(one[:], 1.0)
@@ -54,7 +53,6 @@ def tile_list_quote_smoothing_kernel(
         for a in range(PASSES):
             nc.vector.memset(v_plane[a][:].bitcast(I32), 0)
         nc.vector.memset(w4_plane[:].bitcast(I32), 0)
-        nc.scalar.activation(warm[:], one[:], ACT.Sigmoid)
 
         nc.sync.dma_start(offsets[:], offs)
         nc.sync.dma_start(

@@ -104,17 +104,19 @@ def tile_list_quote_smoothing_kernel(
         inv_view = inv.rearrange("(q p) j -> p q j", p=P)
         PAIRS = N_TILES // 2
         damp = {}
-        for h in range(HALVES):
-            for g in range(PAIRS):
-                tile = sb("inv%d_%d" % (h, g), [P, 2, HALF], F32)
-                nc.sync.dma_start(tile[:], inv_view[:, 2 * g : 2 * g + 2, h * HALF : (h + 1) * HALF])
-                damp[h, g] = tile[:]
+        held = {}
+        for g in range(PAIRS):
+            tile = sb("inv%d" % g, [P, 2, S], F32)
+            nc.sync.dma_start(tile[:], inv_view[:, 2 * g : 2 * g + 2, :])
+            for h in range(HALVES):
+                held[h, g] = tile[:, :, h * HALF : (h + 1) * HALF]
+                damp[h, g] = sb("damp%d_%d" % (h, g), [P, 2, HALF], F32)[:]
 
         def cast_scalar(out, in_):
             nc.scalar.activation(out, in_, ACT.Copy)
 
         def cast_gpsimd(out, in_):
-            nc.gpsimd.tensor_scalar(out, in_, 1.0, 0.0, ALU.mult, ALU.add)
+            nc.gpsimd.tensor_copy(out, in_)
 
         def cast_vector(out, in_):
             nc.vector.tensor_copy(out, in_)
@@ -183,7 +185,7 @@ def tile_list_quote_smoothing_kernel(
         gate = [[sb("gate%d_%d" % (h, t), [P, HALF], F32) for t in range(PACK)] for h in range(HALVES)]
         fresh = [sb("fresh%d" % h, [P, PACK, HALF], F32) for h in range(HALVES)]
         slow = [sb("slow%d" % h, [P, PACK, HALF], F32) for h in range(HALVES)]
-        smooth = [sb("smooth%d" % h, [P, PACK, HALF], F32) for h in range(HALVES)]
+        smooth = fresh
 
         h_codes = sb("h_codes", [P, S], U32)
         h_plane = sb("h_plane", [P, S], U8)
@@ -198,8 +200,8 @@ def tile_list_quote_smoothing_kernel(
         def fresh_of(h, t, acc):
             nc.vector.tensor_tensor(fresh[h][:, t, :], gate[h][t][:], acc[:], ALU.mult)
 
-        def slow_of(h, t):
-            acc = bank("c%d_%d" % (h, t), t)
+        def slow_of(h, t, slot):
+            acc = bank("c%d_%d" % (h, t), slot)
             for a in range(PASSES):
                 mx_pass(acc, w3_operand, a, t, h)
             nc.vector.scalar_tensor_tensor(slow[h][:, t, :], gate[h][t][:], 1.0, acc[:], ALU.subtract, ALU.mult)
@@ -214,9 +216,9 @@ def tile_list_quote_smoothing_kernel(
             nc.sync.dma_start(h_view[:, pair, h * HALF : (h + 1) * HALF], smooth[h][:, pair, :])
 
         def weave(h):
-            cast_scalar(
-                woven[h][:].rearrange("p (c i t) -> p c t i", i=4, t=PACK),
-                smooth[h][:].rearrange("p t (c i) -> p c t i", i=4),
+            cast_gpsimd(
+                woven[h][:].rearrange("p (c t) -> p c t", t=PACK),
+                smooth[h][:].rearrange("p t c -> p c t"),
             )
 
         def quantize_half(h):
@@ -226,7 +228,7 @@ def tile_list_quote_smoothing_kernel(
 
         def root(h, g):
             flat = damp[h, g]
-            nc.scalar.activation(flat, flat, ACT.Abs_reciprocal_sqrt, bias=one[:])
+            nc.scalar.activation(flat, held[h, g], ACT.Abs_reciprocal_sqrt, bias=one[:])
 
         def square_scalar(h, g):
             flat = damp[h, g]
@@ -244,16 +246,18 @@ def tile_list_quote_smoothing_kernel(
         def damping_by_tile(h, g):
             for i in range(2):
                 part = damp[h, g][:, i, :]
-                nc.scalar.activation(part, part, ACT.Abs_reciprocal_sqrt, bias=one[:])
+                nc.scalar.activation(part, held[h, g][:, i, :], ACT.Abs_reciprocal_sqrt, bias=one[:])
                 nc.scalar.activation(part, part, ACT.Square)
 
-        def adjust(h, g, split=False):
+        def adjust(h, g, split=False, between=None):
             cols = slice(h * HALF, (h + 1) * HALF)
             y = damp[h, g]
             for i in range(2):
                 q = 2 * g + i
                 n0 = q * P
-                acc = bank("d%d_%d" % (h, q), PACK + (h * N_TILES + q) % PACK)
+                if i == 1 and between is not None:
+                    between()
+                acc = bank("d%d_%d" % (h, q), (h * N_TILES + q) % PACK)
                 nc.tensor.matmul_mx(
                     out=acc[:], lhsT=w4_codes[:, n0 : n0 + P].bitcast(FP8X4),
                     lhsT_scale=w4_plane[:, n0 : n0 + P],
@@ -281,51 +285,44 @@ def tile_list_quote_smoothing_kernel(
         for t in range(PACK):
             gate_of(0, t, acc_a[t])
             fresh_of(0, t, acc_b[t])
-        for t in range(PACK):
-            acc = bank("a1_%d" % t, t)
-            for a in range(PASSES):
-                mx_pass(acc, w1_operand, a, t, 1)
-            gate_of(1, t, acc)
-        acc_b = [bank("b1_%d" % t, PACK + t) for t in range(PACK)]
-        for t in range(PACK):
-            for a in range(PASSES):
-                mx_pass(acc_b[t], w2_operand, a, t, 1)
-
-        w3_bf0 = round_weight("w3_bf0", w3_raw[0], cast_vector, "m j t")
-        fresh_of(1, 0, acc_b[0])
-        w3_mx = [quantize_weight("w3_0", w3_bf0)]
+        w3_bf0 = round_weight("w3_bf0", w3_raw[0], cast_gpsimd, "t m j")
         codes = sb("w3_1_codes", [P, H], U32)
         plane = sb("w3_1_plane", [P, H], U8)
-        w3_bf1 = []
-        for u, cast in enumerate((cast_vector, cast_scalar)):
+        halves = []
+        for u, cast in enumerate((cast_scalar, cast_vector)):
             grouped = sb("w3_bf1_%d" % u, [P, 2 * H], BF16)
             cast(
                 grouped[:].rearrange("p (t m j) -> p m j t", t=2, j=PACK),
                 w3_raw[1][:].rearrange("p j (m t) -> p m j t", t=PACK)[:, :, :, 2 * u : 2 * u + 2],
             )
-            w3_bf1.append(grouped)
-        fresh_of(1, 1, acc_b[1])
+            halves.append(grouped)
+        w3_mx = [quantize_weight("w3_0", w3_bf0)]
         for u in range(2):
             cols = slice(2 * u * P, 2 * (u + 1) * P)
-            nc.vector.quantize_mx(out=codes[:, cols].bitcast(FP8X4), scales=plane[:, cols], in_=w3_bf1[u][:])
+            nc.vector.quantize_mx(out=codes[:, cols].bitcast(FP8X4), scales=plane[:, cols], in_=halves[u][:])
         w3_mx.append((codes, plane))
         w3_operand = fp8_operand(w3_mx)
-
-        fresh_of(1, 2, acc_b[2])
-        damping(0, 0)
-        damping(0, 1)
-        root(0, 2)
         for t in range(PACK):
-            slow_of(0, t)
+            acc = bank("a1_%d" % t, t)
+            for a in range(PASSES):
+                mx_pass(acc, w1_operand, a, t, 1)
+            gate_of(1, t, acc)
+        for t in range(PACK):
+            slow_of(0, t, PACK + t)
         smooth_pair(0, 0, True)
         smooth_pair(0, 1, True)
         weave(0)
-        square_scalar(0, 2)
-        fresh_of(1, 3, acc_b[3])
-        for t in range(PACK - 1):
-            slow_of(1, t)
-        quantize_half(0)
-        slow_of(1, PACK - 1)
+        for g in range(PAIRS):
+            damping(0, g)
+        for t in range(PACK):
+            slow_of(1, t, t)
+        for t in range(PACK):
+            acc = bank("b1_%d" % t, PACK + t)
+            for a in range(PASSES):
+                mx_pass(acc, w2_operand, a, t, 1)
+            fresh_of(1, t, acc)
+            if t == PACK - 2:
+                quantize_half(0)
         smooth_pair(1, 0, True)
         smooth_pair(1, 1, True)
         weave(1)
@@ -334,12 +331,11 @@ def tile_list_quote_smoothing_kernel(
         damping_by_tile(1, 2)
         adjust(0, 0)
         adjust(0, 1)
-        quantize_half(1)
+        adjust(0, 2, split=True, between=lambda: quantize_half(1))
         for q in range(QUADS):
             nc.sync.dma_start(
                 out_3[0, 4 * q : 4 * q + 4, :].bitcast(I32), h_plane[32 * q : 32 * q + 4, :].bitcast(I32)
             )
-        adjust(0, 2)
         adjust(1, 0)
         adjust(1, 1)
         adjust(1, 2, split=True)

@@ -172,13 +172,14 @@ def tile_list_quote_smoothing_kernel(
         def bank(name, slot):
             return psum.tile([P, HALF], F32, name=name, tag="bank%d" % slot)
 
-        def mx_pass(acc, operand, a, t, h):
+        def mx_pass(acc, operand, a, t, h, first=None, final=None):
             codes, plane = operand(a, t)
             nc.tensor.matmul_mx(
                 out=acc[:], lhsT=codes, lhsT_scale=plane,
                 rhs=v_codes[a, h][:].bitcast(FP8X4),
                 rhs_scale=v_plane[a][:, h * HALF : (h + 1) * HALF],
-                start=(a == 0), stop=(a == PASSES - 1),
+                start=(a == 0) if first is None else first,
+                stop=(a == PASSES - 1) if final is None else final,
             )
 
         w1_operand = fp8_operand(w1_mx)
@@ -209,17 +210,22 @@ def tile_list_quote_smoothing_kernel(
         def smooth_pair(h, u, on_vector):
             pair = slice(2 * u, 2 * u + 2)
             if on_vector:
-                nc.vector.tensor_tensor(smooth[h][:, pair, :], fresh[h][:, pair, :], slow[h][:, pair, :], ALU.subtract)
+                nc.vector.tensor_tensor(smooth[h][:, pair, :], fresh[h][:, pair, :], slow[h][:, pair, :], ALU.add)
             else:
                 for t in range(2 * u, 2 * u + 2):
                     nc.gpsimd.tensor_tensor(smooth[h][:, t, :], fresh[h][:, t, :], slow[h][:, t, :], ALU.subtract)
             nc.sync.dma_start(h_view[:, pair, h * HALF : (h + 1) * HALF], smooth[h][:, pair, :])
 
-        def weave(h):
+        def weave(h, mid):
             cast_gpsimd(
-                woven[h][:].rearrange("p (c t) -> p c t", t=PACK),
-                smooth[h][:].rearrange("p t c -> p c t"),
+                woven[h][:, PACK * mid :].rearrange("p (c t) -> p c t", t=PACK),
+                smooth[h][:, :, mid:].rearrange("p t c -> p c t"),
             )
+            if mid:
+                cast_scalar(
+                    woven[h][:, : PACK * mid].rearrange("p (c i t) -> p c t i", i=4, t=PACK),
+                    smooth[h][:, :, :mid].rearrange("p t (c i) -> p c t i", i=4),
+                )
 
         def quantize_half(h):
             cols = slice(h * HALF, (h + 1) * HALF)
@@ -285,22 +291,35 @@ def tile_list_quote_smoothing_kernel(
         for t in range(PACK):
             gate_of(0, t, acc_a[t])
             fresh_of(0, t, acc_b[t])
-        w3_bf0 = round_weight("w3_bf0", w3_raw[0], cast_gpsimd, "t m j")
-        codes = sb("w3_1_codes", [P, H], U32)
-        plane = sb("w3_1_plane", [P, H], U8)
-        halves = []
-        for u, cast in enumerate((cast_scalar, cast_vector)):
-            grouped = sb("w3_bf1_%d" % u, [P, 2 * H], BF16)
+        def negate_scalar(out, in_):
+            nc.scalar.activation(out, in_, ACT.Copy, scale=-1.0)
+
+        def negate_vector(out, in_):
+            nc.vector.tensor_scalar(out, in_, -1.0, None, ALU.mult)
+
+        def negate_gpsimd(out, in_):
+            nc.gpsimd.tensor_scalar(out, in_, -1.0, 0.0, ALU.mult, ALU.add)
+
+        def round_pair(a, u, cast, walk):
+            grouped = sb("w3_bf%d_%d" % (a, u), [P, 2 * H], BF16)
             cast(
-                grouped[:].rearrange("p (t m j) -> p m j t", t=2, j=PACK),
-                w3_raw[1][:].rearrange("p j (m t) -> p m j t", t=PACK)[:, :, :, 2 * u : 2 * u + 2],
+                grouped[:].rearrange("p (t m j) -> p " + walk, t=2, j=PACK),
+                w3_raw[a][:].rearrange("p j (m t) -> p t m j", t=PACK)[:, 2 * u : 2 * u + 2].rearrange("p t m j -> p " + walk),
             )
-            halves.append(grouped)
-        w3_mx = [quantize_weight("w3_0", w3_bf0)]
-        for u in range(2):
-            cols = slice(2 * u * P, 2 * (u + 1) * P)
-            nc.vector.quantize_mx(out=codes[:, cols].bitcast(FP8X4), scales=plane[:, cols], in_=halves[u][:])
-        w3_mx.append((codes, plane))
+            return grouped
+
+        w3_bf = [
+            [round_pair(0, 0, negate_vector, "m j t"), round_pair(0, 1, negate_gpsimd, "t m j")],
+            [round_pair(1, 0, negate_vector, "m j t"), round_pair(1, 1, negate_scalar, "m j t")],
+        ]
+        w3_mx = []
+        for a in range(PASSES):
+            codes = sb("w3_%d_codes" % a, [P, H], U32)
+            plane = sb("w3_%d_plane" % a, [P, H], U8)
+            for u in range(2):
+                cols = slice(2 * u * P, 2 * (u + 1) * P)
+                nc.vector.quantize_mx(out=codes[:, cols].bitcast(FP8X4), scales=plane[:, cols], in_=w3_bf[a][u][:])
+            w3_mx.append((codes, plane))
         w3_operand = fp8_operand(w3_mx)
         for t in range(PACK):
             acc = bank("a1_%d" % t, t)
@@ -311,22 +330,36 @@ def tile_list_quote_smoothing_kernel(
             slow_of(0, t, PACK + t)
         smooth_pair(0, 0, True)
         smooth_pair(0, 1, True)
-        weave(0)
+        weave(0, 0)
         for g in range(PAIRS):
             damping(0, g)
-        for t in range(PACK):
-            slow_of(1, t, t)
-        for t in range(PACK):
-            acc = bank("b1_%d" % t, PACK + t)
+        last = PACK - 1
+        cols1 = slice(HALF, S)
+        for t in range(last):
+            minus_c = bank("c1_%d" % t, t)
             for a in range(PASSES):
-                mx_pass(acc, w2_operand, a, t, 1)
-            fresh_of(1, t, acc)
-            if t == PACK - 2:
-                quantize_half(0)
-        smooth_pair(1, 0, True)
-        smooth_pair(1, 1, True)
-        weave(1)
+                mx_pass(minus_c, w3_operand, a, t, 1)
+            spread = bank("b1_%d" % t, PACK + t)
+            for n, (operand, a) in enumerate([(w2_operand, 0), (w2_operand, 1), (w3_operand, 0), (w3_operand, 1)]):
+                mx_pass(spread, operand, a, t, 1, first=(n == 0), final=(n == 3))
+            nc.vector.tensor_tensor(slow[1][:, t, :], gate[1][t][:], spread[:], ALU.mult)
+            if t > 0:
+                finish()
+            def finish(t=t, minus_c=minus_c):
+                nc.vector.tensor_tensor(smooth[1][:, t, :], slow[1][:, t, :], minus_c[:], ALU.subtract)
+                if t == 1:
+                    nc.sync.dma_start(h_view[:, 0:2, cols1], smooth[1][:, 0:2, :])
+        slow_of(1, last, last)
+        finish()
+        acc = bank("b1_%d" % last, PACK + last)
+        for a in range(PASSES):
+            mx_pass(acc, w2_operand, a, last, 1)
+        fresh_of(1, last, acc)
+        quantize_half(0)
+        nc.vector.tensor_tensor(smooth[1][:, last, :], fresh[1][:, last, :], slow[1][:, last, :], ALU.add)
+        nc.sync.dma_start(h_view[:, 2:4, cols1], smooth[1][:, 2:4, :])
         damping(1, 0)
+        weave(1, HALF // 2)
         damping(1, 1)
         damping_by_tile(1, 2)
         adjust(0, 0)

@@ -64,36 +64,41 @@ def tile_list_quote_smoothing_kernel(
                 w2_scales[:, 4 * q : 4 * q + 4, :].bitcast(I32).rearrange("a r e -> r a e"),
             )
 
-        def load_weight(name, w):
-            raws = []
-            for a in range(PASSES):
-                raw = sb("%s_raw%d" % (name, a), [P, PACK, H], F32)
-                nc.sync.dma_start(
-                    raw[:], w[a * K_PASS : (a + 1) * K_PASS, :].rearrange("(p j) c -> p j c", j=PACK)
-                )
-                raws.append(raw)
-            return raws
+        def load_weight(name, w, a):
+            raw = sb("%s_raw%d" % (name, a), [P, PACK, H], F32)
+            nc.sync.dma_start(
+                raw[:], w[a * K_PASS : (a + 1) * K_PASS, :].rearrange("(p j) c -> p j c", j=PACK)
+            )
+            return raw
 
         w2_raw = sb("w2_raw", [P, PASSES * 2 * H], U8)
         nc.sync.dma_start(
             w2_raw[:].bitcast(I32).rearrange("p (a e) -> p a e", a=PASSES),
             w2_words.bitcast(I32).rearrange("a p e -> p a e"),
         )
-        w1_raw = load_weight("w1", w1)
         picked_rows = sb("picked_rows", [P, S], U8)
         nc.vector.tensor_copy(picked_rows[:], tab_rows[:].indirect(offsets[:]))
-        table = []
-        for a in range(PASSES):
+
+        def load_table(a):
             tile = sb("table%d" % a, [P, T], I32)
             nc.sync.dma_start(tile[:], tab_words[a].rearrange("p n i -> p (n i)").bitcast(I32))
-            table.append(tile)
+            return tile
+
+        def move_scales(a):
             for q in range(QUADS):
                 row = 16 * a + 4 * q
                 nc.sync.dma_start(
                     v_plane[a][32 * q : 32 * q + 4, :].bitcast(I32),
                     picked_rows[row : row + 4, :].bitcast(I32),
                 )
-        w3_raw = load_weight("w3", w3)
+
+        w1_raw = [load_weight("w1", w1, 0)]
+        table = [load_table(0)]
+        move_scales(0)
+        w1_raw.append(load_weight("w1", w1, 1))
+        move_scales(1)
+        table.append(load_table(1))
+        w3_raw = [load_weight("w3", w3, a) for a in range(PASSES)]
         w4_codes = sb("w4_codes", [P, N], I32)
         nc.sync.dma_start(w4_codes[:], w4_words[0].rearrange("p n i -> p (n i)").bitcast(I32))
         for q in range(QUADS):
@@ -309,7 +314,7 @@ def tile_list_quote_smoothing_kernel(
             return grouped
 
         w3_bf = [
-            [round_pair(0, 0, negate_vector, "m j t"), round_pair(0, 1, negate_gpsimd, "t m j")],
+            [round_pair(0, 0, negate_scalar, "m j t"), round_pair(0, 1, negate_gpsimd, "t m j")],
             [round_pair(1, 0, negate_vector, "m j t"), round_pair(1, 1, negate_scalar, "m j t")],
         ]
         w3_mx = []
@@ -328,7 +333,9 @@ def tile_list_quote_smoothing_kernel(
             gate_of(1, t, acc)
         for t in range(PACK):
             slow_of(0, t, PACK + t)
-        smooth_pair(0, 0, True)
+        nc.gpsimd.tensor_tensor(smooth[0][:, 0, :], fresh[0][:, 0, :], slow[0][:, 0, :], ALU.add)
+        nc.vector.tensor_tensor(smooth[0][:, 1, :], fresh[0][:, 1, :], slow[0][:, 1, :], ALU.add)
+        nc.sync.dma_start(h_view[:, 0:2, 0:HALF], smooth[0][:, 0:2, :])
         smooth_pair(0, 1, True)
         weave(0, 0)
         for g in range(PAIRS):

@@ -24,6 +24,8 @@ QUADS = 4
 HALF = 512
 HALVES = S // HALF
 N_TILES = N // P
+W4_ROW = 4
+H_ROW = 12
 
 
 def tile_list_quote_smoothing_kernel(
@@ -103,19 +105,17 @@ def tile_list_quote_smoothing_kernel(
         nc.sync.dma_start(w4_codes[:], w4_words[0].rearrange("p n i -> p (n i)").bitcast(I32))
         for q in range(QUADS):
             nc.sync.dma_start(
-                w4_plane[32 * q : 32 * q + 4, :].bitcast(I32),
+                w4_plane[32 * q + W4_ROW : 32 * q + W4_ROW + 4, :].bitcast(I32),
                 w4_scales[0, 4 * q : 4 * q + 4, :].bitcast(I32),
             )
         inv_view = inv.rearrange("(q p) j -> p q j", p=P)
-        PAIRS = N_TILES // 2
-        damp = {}
-        held = {}
-        for g in range(PAIRS):
-            tile = sb("inv%d" % g, [P, 2, S], F32)
-            nc.sync.dma_start(tile[:], inv_view[:, 2 * g : 2 * g + 2, :])
-            for h in range(HALVES):
-                held[h, g] = tile[:, :, h * HALF : (h + 1) * HALF]
-                damp[h, g] = sb("damp%d_%d" % (h, g), [P, 2, HALF], F32)[:]
+        TRIPLE = 2
+        held = []
+        for g in range(3):
+            tile = sb("inv%d" % g, [P, TRIPLE, S], F32)
+            nc.sync.dma_start(tile[:], inv_view[:, TRIPLE * g : TRIPLE * (g + 1), :])
+            held.append(tile)
+        damp = [sb("damp%d" % h, [P, N_TILES, HALF], F32) for h in range(HALVES)]
 
         def cast_scalar(out, in_):
             nc.scalar.activation(out, in_, ACT.Copy)
@@ -234,52 +234,35 @@ def tile_list_quote_smoothing_kernel(
 
         def quantize_half(h):
             cols = slice(h * HALF, (h + 1) * HALF)
-            nc.vector.quantize_mx(out=h_codes[:, cols].bitcast(FP8X4), scales=h_plane[:, cols], in_=woven[h][:])
+            nc.vector.quantize_mx(out=h_codes[:, cols].bitcast(FP8X4), scales=h_plane[H_ROW:, cols], in_=woven[h][:])
             nc.sync.dma_start(words_view[:, cols], h_codes[:, cols].bitcast(I32))
 
-        def root(h, g):
-            flat = damp[h, g]
-            nc.scalar.activation(flat, held[h, g], ACT.Abs_reciprocal_sqrt, bias=one[:])
+        def root(h, q0, q1):
+            g, i = divmod(q0, TRIPLE)
+            source = held[g][:, i : i + q1 - q0, h * HALF : (h + 1) * HALF]
+            nc.scalar.activation(damp[h][:, q0:q1, :], source, ACT.Abs_reciprocal_sqrt, bias=one[:])
 
-        def square_scalar(h, g):
-            flat = damp[h, g]
-            nc.scalar.activation(flat, flat, ACT.Square)
+        def square(h, q0, q1):
+            nc.scalar.activation(damp[h][:, q0:q1, :], damp[h][:, q0:q1, :], ACT.Square)
 
-        def square_gpsimd(h, g):
-            for i in range(2):
-                part = damp[h, g][:, i, :]
-                nc.gpsimd.tensor_tensor(part, part, part, ALU.mult)
+        def damping(h, q0, q1):
+            root(h, q0, q1)
+            square(h, q0, q1)
 
-        def damping(h, g):
-            root(h, g)
-            square_scalar(h, g)
-
-        def damping_by_tile(h, g):
-            for i in range(2):
-                part = damp[h, g][:, i, :]
-                nc.scalar.activation(part, held[h, g][:, i, :], ACT.Abs_reciprocal_sqrt, bias=one[:])
-                nc.scalar.activation(part, part, ACT.Square)
-
-        def adjust(h, g, split=False, between=None):
+        def adjust(h, q):
             cols = slice(h * HALF, (h + 1) * HALF)
-            y = damp[h, g]
-            for i in range(2):
-                q = 2 * g + i
-                n0 = q * P
-                if i == 1 and between is not None:
-                    between()
-                acc = bank("d%d_%d" % (h, q), (h * N_TILES + q) % PACK)
-                nc.tensor.matmul_mx(
-                    out=acc[:], lhsT=w4_codes[:, n0 : n0 + P].bitcast(FP8X4),
-                    lhsT_scale=w4_plane[:, n0 : n0 + P],
-                    rhs=h_codes[:, cols].bitcast(FP8X4), rhs_scale=h_plane[:, cols],
-                    start=True, stop=True,
-                )
-                nc.vector.tensor_tensor(y[:, i, :], y[:, i, :], acc[:], ALU.mult)
-                if split:
-                    nc.sync.dma_start(y_view[:, q, cols], y[:, i, :])
-            if not split:
-                nc.sync.dma_start(y_view[:, 2 * g : 2 * g + 2, cols], y)
+            n0 = q * P
+            acc = bank("d%d_%d" % (h, q), (h * N_TILES + q) % PACK)
+            nc.tensor.matmul_mx(
+                out=acc[:], lhsT=w4_codes[:, n0 : n0 + P].bitcast(FP8X4),
+                lhsT_scale=w4_plane[W4_ROW:, n0 : n0 + P],
+                rhs=h_codes[:, cols].bitcast(FP8X4), rhs_scale=h_plane[H_ROW:, cols],
+                start=True, stop=True,
+            )
+            nc.vector.tensor_tensor(damp[h][:, q, :], damp[h][:, q, :], acc[:], ALU.mult)
+
+        def store_y(h, q0, q1):
+            nc.sync.dma_start(y_view[:, q0:q1, h * HALF : (h + 1) * HALF], damp[h][:, q0:q1, :])
 
         gather(0, 0)
         gather(0, 1)
@@ -335,11 +318,11 @@ def tile_list_quote_smoothing_kernel(
             slow_of(0, t, PACK + t)
         nc.gpsimd.tensor_tensor(smooth[0][:, 0, :], fresh[0][:, 0, :], slow[0][:, 0, :], ALU.add)
         nc.vector.tensor_tensor(smooth[0][:, 1, :], fresh[0][:, 1, :], slow[0][:, 1, :], ALU.add)
-        nc.sync.dma_start(h_view[:, 0:2, 0:HALF], smooth[0][:, 0:2, :])
-        smooth_pair(0, 1, True)
+        nc.vector.tensor_tensor(smooth[0][:, 2:4, :], fresh[0][:, 2:4, :], slow[0][:, 2:4, :], ALU.add)
+        nc.sync.dma_start(h_view[:, :, 0:HALF], smooth[0][:])
         weave(0, 0)
-        for g in range(PAIRS):
-            damping(0, g)
+        for q in range(0, N_TILES, 2):
+            damping(0, q, q + 2)
         last = PACK - 1
         cols1 = slice(HALF, S)
         for t in range(last):
@@ -365,17 +348,25 @@ def tile_list_quote_smoothing_kernel(
         quantize_half(0)
         nc.vector.tensor_tensor(smooth[1][:, last, :], fresh[1][:, last, :], slow[1][:, last, :], ALU.add)
         nc.sync.dma_start(h_view[:, 2:4, cols1], smooth[1][:, 2:4, :])
-        damping(1, 0)
+        damping(1, 0, 2)
         weave(1, HALF // 2)
-        damping(1, 1)
-        damping_by_tile(1, 2)
-        adjust(0, 0)
-        adjust(0, 1)
-        adjust(0, 2, split=True, between=lambda: quantize_half(1))
+        damping(1, 2, 4)
+        damping(1, 4, 5)
+        damping(1, 5, 6)
+        for q in range(N_TILES):
+            if q == N_TILES - 1:
+                quantize_half(1)
+            adjust(0, q)
+            if q % 3 == 2:
+                store_y(0, q - 2, q + 1)
         for q in range(QUADS):
             nc.sync.dma_start(
-                out_3[0, 4 * q : 4 * q + 4, :].bitcast(I32), h_plane[32 * q : 32 * q + 4, :].bitcast(I32)
+                out_3[0, 4 * q : 4 * q + 4, :].bitcast(I32),
+                h_plane[32 * q + H_ROW : 32 * q + H_ROW + 4, :].bitcast(I32),
             )
-        adjust(1, 0)
-        adjust(1, 1)
-        adjust(1, 2, split=True)
+        for q in range(N_TILES):
+            adjust(1, q)
+            if q in (1, 3):
+                store_y(1, q - 1, q + 1)
+            elif q > 3:
+                store_y(1, q, q + 1)

@@ -288,17 +288,25 @@ def tile_list_quote_smoothing_kernel(
         def negate_gpsimd(out, in_):
             nc.gpsimd.tensor_scalar(out, in_, -1.0, 0.0, ALU.mult, ALU.add)
 
-        def round_pair(a, u, cast, walk):
+        def round_pair(a, u, shares):
             grouped = sb("w3_bf%d_%d" % (a, u), [P, 2 * H], BF16)
-            cast(
-                grouped[:].rearrange("p (t m j) -> p " + walk, t=2, j=PACK),
-                w3_raw[a][:].rearrange("p j (m t) -> p t m j", t=PACK)[:, 2 * u : 2 * u + 2].rearrange("p t m j -> p " + walk),
-            )
+            out = grouped[:].rearrange("p (t m j) -> p t m j", t=2, j=PACK)
+            raw = w3_raw[a][:].rearrange("p j (m t) -> p t m j", t=PACK)[:, 2 * u : 2 * u + 2]
+            for cast, walk, columns in shares:
+                order = "p t m j -> p " + walk
+                cast(out[:, :, columns, :].rearrange(order), raw[:, :, columns, :].rearrange(order))
             return grouped
 
+        whole, low, high = slice(0, P), slice(0, P // 2), slice(P // 2, P)
         w3_bf = [
-            [round_pair(0, 0, negate_scalar, "m j t"), round_pair(0, 1, negate_gpsimd, "t m j")],
-            [round_pair(1, 0, negate_vector, "m j t"), round_pair(1, 1, negate_scalar, "m j t")],
+            [
+                round_pair(0, 0, [(negate_scalar, "m j t", low), (negate_vector, "m j t", high)]),
+                round_pair(0, 1, [(negate_gpsimd, "t m j", whole)]),
+            ],
+            [
+                round_pair(1, 0, [(negate_vector, "m j t", whole)]),
+                round_pair(1, 1, [(negate_scalar, "m j t", whole)]),
+            ],
         ]
         w3_mx = []
         for a in range(PASSES):
@@ -349,7 +357,7 @@ def tile_list_quote_smoothing_kernel(
         nc.vector.tensor_tensor(smooth[1][:, last, :], fresh[1][:, last, :], slow[1][:, last, :], ALU.add)
         nc.sync.dma_start(h_view[:, 2:4, cols1], smooth[1][:, 2:4, :])
         damping(1, 0, 2)
-        weave(1, HALF // 2)
+        weave(1, 224)
         damping(1, 2, 4)
         damping(1, 4, 5)
         damping(1, 5, 6)

@@ -81,10 +81,11 @@ def tile_list_quote_smoothing_kernel(
         picked_rows = sb("picked_rows", [P, S], U8)
         nc.vector.tensor_copy(picked_rows[:], tab_rows[:].indirect(offsets[:]))
 
-        def load_table(a):
-            tile = sb("table%d" % a, [P, T], I32)
-            nc.sync.dma_start(tile[:], tab_words[a].rearrange("p n i -> p (n i)").bitcast(I32))
-            return tile
+        table = [sb("table%d" % a, [P, T], I32) for a in range(PASSES)]
+
+        def load_table(a, cols):
+            words = tab_words[a].rearrange("p n i -> p (n i)").bitcast(I32)
+            nc.sync.dma_start(table[a][:, cols], words[:, cols])
 
         def move_scales(a):
             for q in range(QUADS):
@@ -94,12 +95,12 @@ def tile_list_quote_smoothing_kernel(
                     picked_rows[row : row + 4, :].bitcast(I32),
                 )
 
-        w1_raw = [load_weight("w1", w1, 0)]
-        table = [load_table(0)]
+        w1_raw = [load_weight("w1", w1, a) for a in range(PASSES)]
+        load_table(0, slice(0, T // 4))
         move_scales(0)
-        w1_raw.append(load_weight("w1", w1, 1))
+        load_table(0, slice(T // 4, T))
         move_scales(1)
-        table.append(load_table(1))
+        load_table(1, slice(0, T))
         w3_raw = [load_weight("w3", w3, a) for a in range(PASSES)]
         w4_codes = sb("w4_codes", [P, N], I32)
         nc.sync.dma_start(w4_codes[:], w4_words[0].rearrange("p n i -> p (n i)").bitcast(I32))

@@ -56,6 +56,8 @@ def tile_list_quote_smoothing_kernel(
             nc.vector.memset(v_plane[a][:].bitcast(I32), 0)
         nc.vector.memset(w4_plane[:].bitcast(I32), 0)
 
+        warm = sb("warm", [P, 1], F32)
+        nc.scalar.activation(warm[:], one[:], ACT.Sigmoid)
         nc.sync.dma_start(offsets[:], offs)
         nc.sync.dma_start(
             tab_rows[0:32, :].bitcast(I32), tab_scales.rearrange("a q t -> (a q) t").bitcast(I32)
@@ -95,20 +97,14 @@ def tile_list_quote_smoothing_kernel(
                     picked_rows[row : row + 4, :].bitcast(I32),
                 )
 
-        w1_raw = [load_weight("w1", w1, a) for a in range(PASSES)]
-        load_table(0, slice(0, T // 4))
+        w1_raw = [load_weight("w1", w1, 0)]
+        load_table(0, slice(0, T))
         move_scales(0)
-        load_table(0, slice(T // 4, T))
+        load_table(1, slice(0, T // 2))
         move_scales(1)
-        load_table(1, slice(0, T))
+        load_table(1, slice(T // 2, T))
+        w1_raw.append(load_weight("w1", w1, 1))
         w3_raw = [load_weight("w3", w3, a) for a in range(PASSES)]
-        w4_codes = sb("w4_codes", [P, N], I32)
-        nc.sync.dma_start(w4_codes[:], w4_words[0].rearrange("p n i -> p (n i)").bitcast(I32))
-        for q in range(QUADS):
-            nc.sync.dma_start(
-                w4_plane[32 * q + W4_ROW : 32 * q + W4_ROW + 4, :].bitcast(I32),
-                w4_scales[0, 4 * q : 4 * q + 4, :].bitcast(I32),
-            )
         inv_view = inv.rearrange("(q p) j -> p q j", p=P)
         TRIPLE = 2
         held = []
@@ -116,7 +112,26 @@ def tile_list_quote_smoothing_kernel(
             tile = sb("inv%d" % g, [P, TRIPLE, S], F32)
             nc.sync.dma_start(tile[:], inv_view[:, TRIPLE * g : TRIPLE * (g + 1), :])
             held.append(tile)
-        damp = [sb("damp%d" % h, [P, N_TILES, HALF], F32) for h in range(HALVES)]
+        w4_codes = sb("w4_codes", [P, N], I32)
+        nc.sync.dma_start(w4_codes[:], w4_words[0].rearrange("p n i -> p (n i)").bitcast(I32))
+        for q in range(QUADS):
+            nc.sync.dma_start(
+                w4_plane[32 * q + W4_ROW : 32 * q + W4_ROW + 4, :].bitcast(I32),
+                w4_scales[0, 4 * q : 4 * q + 4, :].bitcast(I32),
+            )
+        damp0 = sb("damp0", [P, N_TILES, HALF], F32)
+        spare = sb("spare", [P, 2, HALF], F32)
+        damp_last = sb("damp_last", [P, 2, HALF], F32)
+        pairs = [
+            [damp0[:, 0:2, :], damp0[:, 2:4, :], damp0[:, 4:6, :]],
+            [held[2][:, :, 0:HALF], spare[:], damp_last[:]],
+        ]
+
+        def damp(h, q0, q1):
+            if h == 0:
+                return damp0[:, q0:q1, :]
+            g, i = divmod(q0, 2)
+            return pairs[h][g][:, i : i + q1 - q0, :]
 
         def cast_scalar(out, in_):
             nc.scalar.activation(out, in_, ACT.Copy)
@@ -141,7 +156,7 @@ def tile_list_quote_smoothing_kernel(
             nc.vector.quantize_mx(out=codes[:].bitcast(FP8X4), scales=plane[:], in_=grouped[:])
             return codes, plane
 
-        w1_bf = [round_weight("w1_bf%d" % a, w1_raw[a], cast_scalar, "m j t") for a in range(PASSES)]
+        w1_bf = round_weight("w1_bf0", w1_raw[0], cast_scalar, "m j t")
 
         w2_codes = sb("w2_codes", [P, PASSES * 2 * H], U8)
         nc.vector.tensor_copy(
@@ -153,7 +168,7 @@ def tile_list_quote_smoothing_kernel(
             w2_plane[:].rearrange("p (a t m) -> p a t m", a=PASSES, t=PACK),
             w2_rows[:].rearrange("p (a m t) -> p a t m", a=PASSES, t=PACK),
         )
-        w1_mx = [quantize_weight("w1_%d" % a, w1_bf[a]) for a in range(PASSES)]
+        w1_mx = [quantize_weight("w1_0", w1_bf)]
 
         v_codes = {}
 
@@ -238,48 +253,36 @@ def tile_list_quote_smoothing_kernel(
             nc.vector.quantize_mx(out=h_codes[:, cols].bitcast(FP8X4), scales=h_plane[H_ROW:, cols], in_=woven[h][:])
             nc.sync.dma_start(words_view[:, cols], h_codes[:, cols].bitcast(I32))
 
-        def root(h, q0, q1):
+        def damping(h, q0, q1):
             g, i = divmod(q0, TRIPLE)
             source = held[g][:, i : i + q1 - q0, h * HALF : (h + 1) * HALF]
-            nc.scalar.activation(damp[h][:, q0:q1, :], source, ACT.Abs_reciprocal_sqrt, bias=one[:])
-
-        def square(h, q0, q1):
-            nc.scalar.activation(damp[h][:, q0:q1, :], damp[h][:, q0:q1, :], ACT.Square)
-
-        def damping(h, q0, q1):
-            root(h, q0, q1)
-            square(h, q0, q1)
+            roots = spare[:] if (h, q0) == (0, 4) else damp(h, q0, q1)
+            nc.scalar.activation(roots, source, ACT.Abs_reciprocal_sqrt, bias=one[:])
+            nc.scalar.activation(damp(h, q0, q1), roots, ACT.Square)
 
         def adjust(h, q):
             cols = slice(h * HALF, (h + 1) * HALF)
             n0 = q * P
-            acc = bank("d%d_%d" % (h, q), (h * N_TILES + q) % PACK)
+            acc = bank("d%d_%d" % (h, q), (1 + h * N_TILES + q) % 8)
             nc.tensor.matmul_mx(
                 out=acc[:], lhsT=w4_codes[:, n0 : n0 + P].bitcast(FP8X4),
                 lhsT_scale=w4_plane[W4_ROW:, n0 : n0 + P],
                 rhs=h_codes[:, cols].bitcast(FP8X4), rhs_scale=h_plane[H_ROW:, cols],
                 start=True, stop=True,
             )
-            nc.vector.tensor_tensor(damp[h][:, q, :], damp[h][:, q, :], acc[:], ALU.mult)
+            nc.vector.tensor_tensor(damp(h, q, q + 1)[:, 0, :], damp(h, q, q + 1)[:, 0, :], acc[:], ALU.mult)
 
         def store_y(h, q0, q1):
-            nc.sync.dma_start(y_view[:, q0:q1, h * HALF : (h + 1) * HALF], damp[h][:, q0:q1, :])
+            nc.sync.dma_start(y_view[:, q0:q1, h * HALF : (h + 1) * HALF], damp(h, q0, q1))
 
         gather(0, 0)
         gather(0, 1)
+        last = PACK - 1
         acc_a = [bank("a0_%d" % t, t) for t in range(PACK)]
         acc_b = [bank("b0_%d" % t, PACK + t) for t in range(PACK)]
         for t in range(PACK):
             mx_pass(acc_a[t], w1_operand, 0, t, 0)
-            mx_pass(acc_b[t], w2_operand, 0, t, 0)
-        gather(1, 0)
-        gather(1, 1)
-        for t in range(PACK):
-            mx_pass(acc_a[t], w1_operand, 1, t, 0)
-            mx_pass(acc_b[t], w2_operand, 1, t, 0)
-        for t in range(PACK):
-            gate_of(0, t, acc_a[t])
-            fresh_of(0, t, acc_b[t])
+            mx_pass(acc_b[t], w2_operand, 0, t, 0, first=True, final=False)
         def negate_scalar(out, in_):
             nc.scalar.activation(out, in_, ACT.Copy, scale=-1.0)
 
@@ -289,14 +292,33 @@ def tile_list_quote_smoothing_kernel(
         def negate_gpsimd(out, in_):
             nc.gpsimd.tensor_scalar(out, in_, -1.0, 0.0, ALU.mult, ALU.add)
 
-        def round_pair(a, u, shares):
-            grouped = sb("w3_bf%d_%d" % (a, u), [P, 2 * H], BF16)
+        def round_pair(a, u, shares, name="w3", source=None):
+            grouped = sb("%s_bf%d_%d" % (name, a, u), [P, 2 * H], BF16)
             out = grouped[:].rearrange("p (t m j) -> p t m j", t=2, j=PACK)
-            raw = w3_raw[a][:].rearrange("p j (m t) -> p t m j", t=PACK)[:, 2 * u : 2 * u + 2]
+            raw = (source or w3_raw)[a][:].rearrange("p j (m t) -> p t m j", t=PACK)[:, 2 * u : 2 * u + 2]
             for cast, walk, columns in shares:
                 order = "p t m j -> p " + walk
                 cast(out[:, :, columns, :].rearrange(order), raw[:, :, columns, :].rearrange(order))
             return grouped
+
+        gather(1, 0)
+        gather(1, 1)
+        for t in range(PACK):
+            mx_pass(acc_b[t], w2_operand, 1, t, 0, first=False, final=(t < last))
+        codes = sb("w1_1_codes", [P, H], U32)
+        plane = sb("w1_1_plane", [P, H], U8)
+        late = [round_pair(1, 0, [(cast_vector, "m j t", slice(0, P))], "w1", w1_raw),
+                round_pair(1, 1, [(cast_scalar, "m j t", slice(0, P))], "w1", w1_raw)]
+        for u in range(2):
+            cols = slice(2 * u * P, 2 * (u + 1) * P)
+            nc.vector.quantize_mx(out=codes[:, cols].bitcast(FP8X4), scales=plane[:, cols], in_=late[u][:])
+        w1_mx.append((codes, plane))
+        for t in range(PACK):
+            mx_pass(acc_a[t], w1_operand, 1, t, 0)
+        for t in range(PACK):
+            gate_of(0, t, acc_a[t])
+            if t < last:
+                fresh_of(0, t, acc_b[t])
 
         whole, low, high = slice(0, P), slice(0, P // 2), slice(P // 2, P)
         w3_bf = [
@@ -323,51 +345,67 @@ def tile_list_quote_smoothing_kernel(
             for a in range(PASSES):
                 mx_pass(acc, w1_operand, a, t, 1)
             gate_of(1, t, acc)
-        for t in range(PACK):
-            slow_of(0, t, PACK + t)
-        nc.gpsimd.tensor_tensor(smooth[0][:, 0, :], fresh[0][:, 0, :], slow[0][:, 0, :], ALU.add)
-        nc.vector.tensor_tensor(smooth[0][:, 1, :], fresh[0][:, 1, :], slow[0][:, 1, :], ALU.add)
-        nc.vector.tensor_tensor(smooth[0][:, 2:4, :], fresh[0][:, 2:4, :], slow[0][:, 2:4, :], ALU.add)
-        nc.sync.dma_start(h_view[:, :, 0:HALF], smooth[0][:])
+
+        def add_gpsimd(h, t):
+            nc.gpsimd.tensor_tensor(smooth[h][:, t, :], fresh[h][:, t, :], slow[h][:, t, :], ALU.add)
+
+        def gated(h, t, spread):
+            nc.vector.tensor_tensor(slow[h][:, t, :], gate[h][t][:], spread[:], ALU.mult)
+
+        def finish(h, t, minus_c):
+            nc.vector.tensor_tensor(smooth[h][:, t, :], slow[h][:, t, :], minus_c[:], ALU.subtract)
+
+        def product(name, slot, terms, t, h):
+            acc = bank(name, slot)
+            for n, (operand, a) in enumerate(terms):
+                mx_pass(acc, operand, a, t, h, first=(n == 0), final=(n == len(terms) - 1))
+            return acc
+
+        b_terms = [(w2_operand, a) for a in range(PASSES)]
+        c_terms = [(w3_operand, a) for a in range(PASSES)]
+        cols0, cols1 = slice(0, HALF), slice(HALF, S)
+
+        slow_of(0, 0, PACK)
+        add_gpsimd(0, 0)
+        for a in range(PASSES):
+            mx_pass(acc_b[last], w3_operand, a, last, 0, first=False, final=(a == PASSES - 1))
+        slow_of(0, 1, PACK + 1)
+        add_gpsimd(0, 1)
+        slow_of(0, 2, PACK + 2)
+        add_gpsimd(0, 2)
+        gated(0, last, acc_b[last])
+        minus_c = product("c0_3", 0, c_terms, last, 0)
+        spread0 = product("e1_0", PACK, b_terms + c_terms, 0, 1)
+        gated(1, 0, spread0)
+        finish(0, last, minus_c)
+        nc.sync.dma_start(h_view[:, :, cols0], smooth[0][:])
         weave(0, 0)
         for q in range(0, N_TILES, 2):
             damping(0, q, q + 2)
-        last = PACK - 1
-        cols1 = slice(HALF, S)
-        for t in range(last):
-            minus_c = bank("c1_%d" % t, t)
-            for a in range(PASSES):
-                mx_pass(minus_c, w3_operand, a, t, 1)
-            spread = bank("b1_%d" % t, PACK + t)
-            for n, (operand, a) in enumerate([(w2_operand, 0), (w2_operand, 1), (w3_operand, 0), (w3_operand, 1)]):
-                mx_pass(spread, operand, a, t, 1, first=(n == 0), final=(n == 3))
-            nc.vector.tensor_tensor(slow[1][:, t, :], gate[1][t][:], spread[:], ALU.mult)
-            if t > 0:
-                finish()
-            def finish(t=t, minus_c=minus_c):
-                nc.vector.tensor_tensor(smooth[1][:, t, :], slow[1][:, t, :], minus_c[:], ALU.subtract)
-                if t == 1:
-                    nc.sync.dma_start(h_view[:, 0:2, cols1], smooth[1][:, 0:2, :])
-        slow_of(1, last, last)
-        finish()
-        acc = bank("b1_%d" % last, PACK + last)
-        for a in range(PASSES):
-            mx_pass(acc, w2_operand, a, last, 1)
-        fresh_of(1, last, acc)
+        c0 = product("c1_0", 1, c_terms, 0, 1)
+        spread1 = product("e1_1", PACK + 1, b_terms + c_terms, 1, 1)
+        gated(1, 1, spread1)
+        finish(1, 0, c0)
+        c1 = product("c1_1", 2, c_terms, 1, 1)
+        fresh_of(1, 2, product("b1_2", PACK + 2, b_terms, 2, 1))
+        finish(1, 1, c1)
+        nc.sync.dma_start(h_view[:, 0:2, cols1], smooth[1][:, 0:2, :])
+        slow_of(1, 2, 3)
+        fresh_of(1, 3, product("b1_3", PACK + 3, b_terms, 3, 1))
+        slow_of(1, 3, 0)
         quantize_half(0)
-        nc.vector.tensor_tensor(smooth[1][:, last, :], fresh[1][:, last, :], slow[1][:, last, :], ALU.add)
+        nc.vector.tensor_tensor(smooth[1][:, 2:4, :], fresh[1][:, 2:4, :], slow[1][:, 2:4, :], ALU.add)
         nc.sync.dma_start(h_view[:, 2:4, cols1], smooth[1][:, 2:4, :])
         damping(1, 0, 2)
-        weave(1, 224)
+        weave(1, 0)
         damping(1, 2, 4)
         damping(1, 4, 5)
         damping(1, 5, 6)
         for q in range(N_TILES):
-            if q == N_TILES - 1:
-                quantize_half(1)
             adjust(0, q)
             if q % 3 == 2:
                 store_y(0, q - 2, q + 1)
+        quantize_half(1)
         for q in range(QUADS):
             nc.sync.dma_start(
                 out_3[0, 4 * q : 4 * q + 4, :].bitcast(I32),

@@ -120,18 +120,13 @@ def tile_list_quote_smoothing_kernel(
                 w4_scales[0, 4 * q : 4 * q + 4, :].bitcast(I32),
             )
         damp0 = sb("damp0", [P, N_TILES, HALF], F32)
-        spare = sb("spare", [P, 2, HALF], F32)
-        damp_last = sb("damp_last", [P, 2, HALF], F32)
-        pairs = [
-            [damp0[:, 0:2, :], damp0[:, 2:4, :], damp0[:, 4:6, :]],
-            [held[2][:, :, 0:HALF], spare[:], damp_last[:]],
-        ]
+        late_fresh = sb("late_fresh", [P, 2, HALF], F32)
 
         def damp(h, q0, q1):
             if h == 0:
                 return damp0[:, q0:q1, :]
             g, i = divmod(q0, 2)
-            return pairs[h][g][:, i : i + q1 - q0, :]
+            return [held[2][:, :, 0:HALF], slow[1][:, 2:4, :], late_fresh[:]][g][:, i : i + q1 - q0, :]
 
         def cast_scalar(out, in_):
             nc.scalar.activation(out, in_, ACT.Copy)
@@ -220,7 +215,8 @@ def tile_list_quote_smoothing_kernel(
             nc.scalar.activation(gate[h][t][:], acc[:], ACT.Sigmoid)
 
         def fresh_of(h, t, acc):
-            nc.vector.tensor_tensor(fresh[h][:, t, :], gate[h][t][:], acc[:], ALU.mult)
+            out = fresh[h][:, t, :] if h == 0 else late_fresh[:, t - 2, :]
+            nc.vector.tensor_tensor(out, gate[h][t][:], acc[:], ALU.mult)
 
         def slow_of(h, t, slot):
             acc = bank("c%d_%d" % (h, t), slot)
@@ -256,7 +252,8 @@ def tile_list_quote_smoothing_kernel(
         def damping(h, q0, q1):
             g, i = divmod(q0, TRIPLE)
             source = held[g][:, i : i + q1 - q0, h * HALF : (h + 1) * HALF]
-            roots = spare[:] if (h, q0) == (0, 4) else damp(h, q0, q1)
+            spare = woven[1][:].bitcast(F32).rearrange("p (q c) -> p q c", q=2)
+            roots = spare if (h, q0) == (0, 4) else damp(h, q0, q1)
             nc.scalar.activation(roots, source, ACT.Abs_reciprocal_sqrt, bias=one[:])
             nc.scalar.activation(damp(h, q0, q1), roots, ACT.Square)
 
@@ -324,7 +321,7 @@ def tile_list_quote_smoothing_kernel(
         w3_bf = [
             [
                 round_pair(0, 0, [(negate_scalar, "m j t", low), (negate_vector, "m j t", high)]),
-                round_pair(0, 1, [(negate_gpsimd, "t m j", whole)]),
+                round_pair(0, 1, [(negate_gpsimd, "m t j", whole)]),
             ],
             [
                 round_pair(1, 0, [(negate_vector, "m j t", whole)]),
@@ -394,10 +391,10 @@ def tile_list_quote_smoothing_kernel(
         fresh_of(1, 3, product("b1_3", PACK + 3, b_terms, 3, 1))
         slow_of(1, 3, 0)
         quantize_half(0)
-        nc.vector.tensor_tensor(smooth[1][:, 2:4, :], fresh[1][:, 2:4, :], slow[1][:, 2:4, :], ALU.add)
+        nc.vector.tensor_tensor(smooth[1][:, 2:4, :], late_fresh[:], slow[1][:, 2:4, :], ALU.add)
         nc.sync.dma_start(h_view[:, 2:4, cols1], smooth[1][:, 2:4, :])
         damping(1, 0, 2)
-        weave(1, 0)
+        weave(1, 160)
         damping(1, 2, 4)
         damping(1, 4, 5)
         damping(1, 5, 6)

@@ -391,8 +391,9 @@ def tile_list_quote_smoothing_kernel(
         fresh_of(1, 3, product("b1_3", PACK + 3, b_terms, 3, 1))
         slow_of(1, 3, 0)
         quantize_half(0)
-        nc.vector.tensor_tensor(smooth[1][:, 2:4, :], late_fresh[:], slow[1][:, 2:4, :], ALU.add)
-        nc.sync.dma_start(h_view[:, 2:4, cols1], smooth[1][:, 2:4, :])
+        for t in (2, 3):
+            nc.vector.tensor_tensor(smooth[1][:, t, :], late_fresh[:, t - 2, :], slow[1][:, t, :], ALU.add)
+            nc.sync.dma_start(h_view[:, t, cols1], smooth[1][:, t, :])
         damping(1, 0, 2)
         weave(1, 160)
         damping(1, 2, 4)
@@ -400,8 +401,10 @@ def tile_list_quote_smoothing_kernel(
         damping(1, 5, 6)
         for q in range(N_TILES):
             adjust(0, q)
-            if q % 3 == 2:
-                store_y(0, q - 2, q + 1)
+            if q < 2:
+                store_y(0, q, q + 1)
+            elif q % 2:
+                store_y(0, q - 1, q + 1)
         quantize_half(1)
         for q in range(QUADS):
             nc.sync.dma_start(

@@ -26,6 +26,7 @@ HALVES = S // HALF
 N_TILES = N // P
 W4_ROW = 4
 H_ROW = 12
+SCALAR_WEAVE = 256
 
 
 def tile_list_quote_smoothing_kernel(
@@ -106,12 +107,16 @@ def tile_list_quote_smoothing_kernel(
         w1_raw.append(load_weight("w1", w1, 1))
         w3_raw = [load_weight("w3", w3, a) for a in range(PASSES)]
         inv_view = inv.rearrange("(q p) j -> p q j", p=P)
-        TRIPLE = 2
-        held = []
-        for g in range(3):
-            tile = sb("inv%d" % g, [P, TRIPLE, S], F32)
-            nc.sync.dma_start(tile[:], inv_view[:, TRIPLE * g : TRIPLE * (g + 1), :])
-            held.append(tile)
+        rows = {}
+
+        def load_inv(q0, q1):
+            tile = sb("inv%d" % q0, [P, q1 - q0, S], F32)
+            nc.sync.dma_start(tile[:], inv_view[:, q0:q1, :])
+            for q in range(q0, q1):
+                rows[q] = tile[:, q - q0, :]
+
+        load_inv(0, 1)
+        load_inv(1, 2)
         w4_codes = sb("w4_codes", [P, N], I32)
         nc.sync.dma_start(w4_codes[:], w4_words[0].rearrange("p n i -> p (n i)").bitcast(I32))
         for q in range(QUADS):
@@ -119,14 +124,8 @@ def tile_list_quote_smoothing_kernel(
                 w4_plane[32 * q + W4_ROW : 32 * q + W4_ROW + 4, :].bitcast(I32),
                 w4_scales[0, 4 * q : 4 * q + 4, :].bitcast(I32),
             )
-        damp0 = sb("damp0", [P, N_TILES, HALF], F32)
-        late_fresh = sb("late_fresh", [P, 2, HALF], F32)
-
-        def damp(h, q0, q1):
-            if h == 0:
-                return damp0[:, q0:q1, :]
-            g, i = divmod(q0, 2)
-            return [held[2][:, :, 0:HALF], slow[1][:, 2:4, :], late_fresh[:]][g][:, i : i + q1 - q0, :]
+        load_inv(2, 4)
+        load_inv(4, 6)
 
         def cast_scalar(out, in_):
             nc.scalar.activation(out, in_, ACT.Copy)
@@ -199,10 +198,19 @@ def tile_list_quote_smoothing_kernel(
             )
 
         w1_operand = fp8_operand(w1_mx)
-        gate = [[sb("gate%d_%d" % (h, t), [P, HALF], F32) for t in range(PACK)] for h in range(HALVES)]
-        fresh = [sb("fresh%d" % h, [P, PACK, HALF], F32) for h in range(HALVES)]
+        gate = {(t, h): sb("gate%d_%d" % (t, h), [P, HALF], F32) for t in range(PACK) for h in range(HALVES)}
+        smooth = [sb("smooth%d" % h, [P, PACK, HALF], F32)[:] for h in range(HALVES)]
+        fresh_second = sb("fresh_second", [P, 2, HALF], F32)
+        front = sb("front", [P, 3 * HALF], F32)
+        fresh_first = front[:, HALF:].rearrange("p (t j) -> p t j", t=2)
+        fresh_last = sb("fresh_last", [P, HALF], F32)
         slow = [sb("slow%d" % h, [P, PACK, HALF], F32) for h in range(HALVES)]
-        smooth = fresh
+
+        def cols(h):
+            return slice(h * HALF, (h + 1) * HALF)
+
+        def smooth_at(t, h):
+            return smooth[h][:, t, :]
 
         h_codes = sb("h_codes", [P, S], U32)
         h_plane = sb("h_plane", [P, S], U8)
@@ -211,77 +219,56 @@ def tile_list_quote_smoothing_kernel(
         y_view = out_0.rearrange("(q p) j -> p q j", p=P)
         woven = [sb("woven%d" % h, [P, PACK * HALF], BF16) for h in range(HALVES)]
 
-        def gate_of(h, t, acc):
-            nc.scalar.activation(gate[h][t][:], acc[:], ACT.Sigmoid)
+        def gate_of(t, h, acc):
+            nc.scalar.activation(gate[t, h][:], acc[:], ACT.Sigmoid)
 
-        def fresh_of(h, t, acc):
-            out = fresh[h][:, t, :] if h == 0 else late_fresh[:, t - 2, :]
-            nc.vector.tensor_tensor(out, gate[h][t][:], acc[:], ALU.mult)
+        def gated(out, t, h, acc):
+            nc.vector.tensor_tensor(out, gate[t, h][:], acc[:], ALU.mult)
 
-        def slow_of(h, t, slot):
-            acc = bank("c%d_%d" % (h, t), slot)
-            for a in range(PASSES):
-                mx_pass(acc, w3_operand, a, t, h)
-            nc.vector.scalar_tensor_tensor(slow[h][:, t, :], gate[h][t][:], 1.0, acc[:], ALU.subtract, ALU.mult)
+        def slow_of(t, h, minus_c):
+            nc.vector.scalar_tensor_tensor(slow[h][:, t, :], gate[t, h][:], 1.0, minus_c[:], ALU.subtract, ALU.mult)
 
-        def smooth_pair(h, u, on_vector):
+        def finish(t, h, minus_c):
+            nc.vector.tensor_tensor(smooth_at(t, h), slow[h][:, t, :], minus_c[:], ALU.subtract)
+
+        def store_h(u, h):
             pair = slice(2 * u, 2 * u + 2)
-            if on_vector:
-                nc.vector.tensor_tensor(smooth[h][:, pair, :], fresh[h][:, pair, :], slow[h][:, pair, :], ALU.add)
-            else:
-                for t in range(2 * u, 2 * u + 2):
-                    nc.gpsimd.tensor_tensor(smooth[h][:, t, :], fresh[h][:, t, :], slow[h][:, t, :], ALU.subtract)
-            nc.sync.dma_start(h_view[:, pair, h * HALF : (h + 1) * HALF], smooth[h][:, pair, :])
+            nc.sync.dma_start(h_view[:, pair, cols(h)], smooth[h][:, pair, :])
 
-        def weave(h, mid):
-            cast_gpsimd(
-                woven[h][:, PACK * mid :].rearrange("p (c t) -> p c t", t=PACK),
-                smooth[h][:, :, mid:].rearrange("p t c -> p c t"),
+        def weave(h, cast, c0, c1):
+            cast(
+                woven[h][:, PACK * c0 : PACK * c1].rearrange("p (c i t) -> p c t i", i=4, t=PACK),
+                smooth[h][:, :, c0:c1].rearrange("p t (c i) -> p c t i", i=4),
             )
-            if mid:
-                cast_scalar(
-                    woven[h][:, : PACK * mid].rearrange("p (c i t) -> p c t i", i=4, t=PACK),
-                    smooth[h][:, :, :mid].rearrange("p t (c i) -> p c t i", i=4),
-                )
 
         def quantize_half(h):
-            cols = slice(h * HALF, (h + 1) * HALF)
-            nc.vector.quantize_mx(out=h_codes[:, cols].bitcast(FP8X4), scales=h_plane[H_ROW:, cols], in_=woven[h][:])
-            nc.sync.dma_start(words_view[:, cols], h_codes[:, cols].bitcast(I32))
+            nc.vector.quantize_mx(out=h_codes[:, cols(h)].bitcast(FP8X4), scales=h_plane[H_ROW:, cols(h)], in_=woven[h][:])
+            nc.sync.dma_start(words_view[:, cols(h)], h_codes[:, cols(h)].bitcast(I32))
 
-        def damping(h, q0, q1):
-            g, i = divmod(q0, TRIPLE)
-            source = held[g][:, i : i + q1 - q0, h * HALF : (h + 1) * HALF]
-            spare = woven[1][:].bitcast(F32).rearrange("p (q c) -> p q c", q=2)
-            roots = spare if (h, q0) == (0, 4) else damp(h, q0, q1)
-            nc.scalar.activation(roots, source, ACT.Abs_reciprocal_sqrt, bias=one[:])
-            nc.scalar.activation(damp(h, q0, q1), roots, ACT.Square)
+        def root(q, span):
+            nc.scalar.activation(rows[q][:, span], rows[q][:, span], ACT.Abs_reciprocal_sqrt, bias=one[:])
 
-        def adjust(h, q):
-            cols = slice(h * HALF, (h + 1) * HALF)
+        def square(q, span):
+            nc.scalar.activation(rows[q][:, span], rows[q][:, span], ACT.Square)
+
+        damp = {(q, h): rows[q][:, cols(h)] for q in range(N_TILES) for h in range(HALVES)}
+
+        def square_gpsimd(q, out=None):
+            source = rows[q][:, cols(0)]
+            if out is not None:
+                damp[q, 0] = out
+            nc.gpsimd.tensor_tensor(damp[q, 0], source, source, ALU.mult)
+
+        def adjust(q, h, slot):
             n0 = q * P
-            acc = bank("d%d_%d" % (h, q), (1 + h * N_TILES + q) % 8)
+            acc = bank("d%d_%d" % (q, h), slot)
             nc.tensor.matmul_mx(
                 out=acc[:], lhsT=w4_codes[:, n0 : n0 + P].bitcast(FP8X4),
                 lhsT_scale=w4_plane[W4_ROW:, n0 : n0 + P],
-                rhs=h_codes[:, cols].bitcast(FP8X4), rhs_scale=h_plane[H_ROW:, cols],
+                rhs=h_codes[:, cols(h)].bitcast(FP8X4), rhs_scale=h_plane[H_ROW:, cols(h)],
                 start=True, stop=True,
             )
-            nc.vector.tensor_tensor(damp(h, q, q + 1)[:, 0, :], damp(h, q, q + 1)[:, 0, :], acc[:], ALU.mult)
-
-        def store_y(h, q0, q1):
-            nc.sync.dma_start(y_view[:, q0:q1, h * HALF : (h + 1) * HALF], damp(h, q0, q1))
-
-        gather(0, 0)
-        gather(0, 1)
-        last = PACK - 1
-        acc_a = [bank("a0_%d" % t, t) for t in range(PACK)]
-        acc_b = [bank("b0_%d" % t, PACK + t) for t in range(PACK)]
-        for t in range(PACK):
-            mx_pass(acc_a[t], w1_operand, 0, t, 0)
-            mx_pass(acc_b[t], w2_operand, 0, t, 0, first=True, final=False)
-        def negate_scalar(out, in_):
-            nc.scalar.activation(out, in_, ACT.Copy, scale=-1.0)
+            nc.vector.tensor_tensor(rows[q][:, cols(h)], damp[q, h], acc[:], ALU.mult)
 
         def negate_vector(out, in_):
             nc.vector.tensor_scalar(out, in_, -1.0, None, ALU.mult)
@@ -289,68 +276,16 @@ def tile_list_quote_smoothing_kernel(
         def negate_gpsimd(out, in_):
             nc.gpsimd.tensor_scalar(out, in_, -1.0, 0.0, ALU.mult, ALU.add)
 
-        def round_pair(a, u, shares, name="w3", source=None):
-            grouped = sb("%s_bf%d_%d" % (name, a, u), [P, 2 * H], BF16)
-            out = grouped[:].rearrange("p (t m j) -> p t m j", t=2, j=PACK)
-            raw = (source or w3_raw)[a][:].rearrange("p j (m t) -> p t m j", t=PACK)[:, 2 * u : 2 * u + 2]
-            for cast, walk, columns in shares:
-                order = "p t m j -> p " + walk
-                cast(out[:, :, columns, :].rearrange(order), raw[:, :, columns, :].rearrange(order))
-            return grouped
+        def round_pair(grouped, raw, slots, cast, walk):
+            out = grouped.rearrange("p (t m j) -> p t m j", t=2, j=PACK)
+            source = raw[:].rearrange("p j (m t) -> p t m j", t=PACK)[:, slots]
+            order = "p t m j -> p " + walk
+            cast(out.rearrange(order), source.rearrange(order))
 
-        gather(1, 0)
-        gather(1, 1)
-        for t in range(PACK):
-            mx_pass(acc_b[t], w2_operand, 1, t, 0, first=False, final=(t < last))
-        codes = sb("w1_1_codes", [P, H], U32)
-        plane = sb("w1_1_plane", [P, H], U8)
-        late = [round_pair(1, 0, [(cast_vector, "m j t", slice(0, P))], "w1", w1_raw),
-                round_pair(1, 1, [(cast_scalar, "m j t", slice(0, P))], "w1", w1_raw)]
-        for u in range(2):
-            cols = slice(2 * u * P, 2 * (u + 1) * P)
-            nc.vector.quantize_mx(out=codes[:, cols].bitcast(FP8X4), scales=plane[:, cols], in_=late[u][:])
-        w1_mx.append((codes, plane))
-        for t in range(PACK):
-            mx_pass(acc_a[t], w1_operand, 1, t, 0)
-        for t in range(PACK):
-            gate_of(0, t, acc_a[t])
-            if t < last:
-                fresh_of(0, t, acc_b[t])
-
-        whole, low, high = slice(0, P), slice(0, P // 2), slice(P // 2, P)
-        w3_bf = [
-            [
-                round_pair(0, 0, [(negate_scalar, "m j t", low), (negate_vector, "m j t", high)]),
-                round_pair(0, 1, [(negate_gpsimd, "m t j", whole)]),
-            ],
-            [
-                round_pair(1, 0, [(negate_vector, "m j t", whole)]),
-                round_pair(1, 1, [(negate_scalar, "m j t", whole)]),
-            ],
-        ]
-        w3_mx = []
-        for a in range(PASSES):
-            codes = sb("w3_%d_codes" % a, [P, H], U32)
-            plane = sb("w3_%d_plane" % a, [P, H], U8)
-            for u in range(2):
-                cols = slice(2 * u * P, 2 * (u + 1) * P)
-                nc.vector.quantize_mx(out=codes[:, cols].bitcast(FP8X4), scales=plane[:, cols], in_=w3_bf[a][u][:])
-            w3_mx.append((codes, plane))
-        w3_operand = fp8_operand(w3_mx)
-        for t in range(PACK):
-            acc = bank("a1_%d" % t, t)
-            for a in range(PASSES):
-                mx_pass(acc, w1_operand, a, t, 1)
-            gate_of(1, t, acc)
-
-        def add_gpsimd(h, t):
-            nc.gpsimd.tensor_tensor(smooth[h][:, t, :], fresh[h][:, t, :], slow[h][:, t, :], ALU.add)
-
-        def gated(h, t, spread):
-            nc.vector.tensor_tensor(slow[h][:, t, :], gate[h][t][:], spread[:], ALU.mult)
-
-        def finish(h, t, minus_c):
-            nc.vector.tensor_tensor(smooth[h][:, t, :], slow[h][:, t, :], minus_c[:], ALU.subtract)
+        def quantize_pair(mx, u, grouped):
+            codes, plane = mx
+            span = slice(2 * u * P, 2 * (u + 1) * P)
+            nc.vector.quantize_mx(out=codes[:, span].bitcast(FP8X4), scales=plane[:, span], in_=grouped)
 
         def product(name, slot, terms, t, h):
             acc = bank(name, slot)
@@ -358,62 +293,105 @@ def tile_list_quote_smoothing_kernel(
                 mx_pass(acc, operand, a, t, h, first=(n == 0), final=(n == len(terms) - 1))
             return acc
 
-        b_terms = [(w2_operand, a) for a in range(PASSES)]
-        c_terms = [(w3_operand, a) for a in range(PASSES)]
-        cols0, cols1 = slice(0, HALF), slice(HALF, S)
+        low, high = slice(0, 2), slice(2, 4)
+        first_tiles = [(0, 0), (1, 0), (0, 1), (1, 1)]
+        second_tiles = [(3, 0), (2, 0), (3, 1), (2, 1)]
 
-        slow_of(0, 0, PACK)
-        add_gpsimd(0, 0)
-        for a in range(PASSES):
-            mx_pass(acc_b[last], w3_operand, a, last, 0, first=False, final=(a == PASSES - 1))
-        slow_of(0, 1, PACK + 1)
-        add_gpsimd(0, 1)
-        slow_of(0, 2, PACK + 2)
-        add_gpsimd(0, 2)
-        gated(0, last, acc_b[last])
-        minus_c = product("c0_3", 0, c_terms, last, 0)
-        spread0 = product("e1_0", PACK, b_terms + c_terms, 0, 1)
-        gated(1, 0, spread0)
-        finish(0, last, minus_c)
-        nc.sync.dma_start(h_view[:, :, cols0], smooth[0][:])
-        weave(0, 0)
-        for q in range(0, N_TILES, 2):
-            damping(0, q, q + 2)
-        c0 = product("c1_0", 1, c_terms, 0, 1)
-        spread1 = product("e1_1", PACK + 1, b_terms + c_terms, 1, 1)
-        gated(1, 1, spread1)
-        finish(1, 0, c0)
-        c1 = product("c1_1", 2, c_terms, 1, 1)
-        fresh_of(1, 2, product("b1_2", PACK + 2, b_terms, 2, 1))
-        finish(1, 1, c1)
-        nc.sync.dma_start(h_view[:, 0:2, cols1], smooth[1][:, 0:2, :])
-        slow_of(1, 2, 3)
-        fresh_of(1, 3, product("b1_3", PACK + 3, b_terms, 3, 1))
-        slow_of(1, 3, 0)
+        gather(0, 0)
+        gather(0, 1)
+        acc_a = {tile: bank("a%d_%d" % tile, n) for n, tile in enumerate(first_tiles)}
+        acc_b = {tile: bank("b%d_%d" % tile, PACK + n) for n, tile in enumerate(first_tiles)}
+        for t, h in first_tiles:
+            mx_pass(acc_a[t, h], w1_operand, 0, t, h)
+            mx_pass(acc_b[t, h], w2_operand, 0, t, h)
+        gather(1, 0)
+        gather(1, 1)
+        for t, h in first_tiles:
+            mx_pass(acc_b[t, h], w2_operand, 1, t, h)
+
+        w1_mx.append((sb("w1_1_codes", [P, H], U32), sb("w1_1_plane", [P, H], U8)))
+        late = [sb("w1_bf1_%d" % u, [P, 2 * H], BF16) for u in range(2)]
+        round_pair(late[0][:], w1_raw[1], low, cast_vector, "m j t")
+        round_pair(late[1][:], w1_raw[1], high, cast_scalar, "m j t")
+        for u in range(2):
+            quantize_pair(w1_mx[1], u, late[u][:])
+        for t, h in first_tiles:
+            mx_pass(acc_a[t, h], w1_operand, 1, t, h)
+        a_terms = [(w1_operand, a) for a in range(PASSES)]
+        b_terms = [(w2_operand, a) for a in range(PASSES)]
+        for t, h in first_tiles:
+            gate_of(t, h, acc_a[t, h])
+        w3_mx = [(sb("w3_%d_codes" % a, [P, H], U32), sb("w3_%d_plane" % a, [P, H], U8)) for a in range(PASSES)]
+        w3_operand = fp8_operand(w3_mx)
+        c_terms = [(w3_operand, a) for a in range(PASSES)]
+        c_late = c_terms[::-1]
+        early = front[:, HALF // 2 : 3 * HALF // 2].bitcast(BF16)
+        staged = front[:, :HALF].bitcast(BF16)
+        round_pair(early, w3_raw[0], low, negate_vector, "m j t")
+        quantize_pair(w3_mx[0], 0, early)
+        round_pair(staged, w3_raw[0], high, negate_gpsimd, "m t j")
+        gated(fresh_first[:, 0, :], 0, 0, acc_b[0, 0])
+        gated(fresh_first[:, 1, :], 1, 0, acc_b[1, 0])
+        gated(fresh_second[:, 0, :], 0, 1, acc_b[0, 1])
+        gated(fresh_second[:, 1, :], 1, 1, acc_b[1, 1])
+        for n, (t, h) in enumerate(second_tiles):
+            gate_of(t, h, product("a%d_%d" % (t, h), n, a_terms, t, h))
+
+        rounded = smooth_at(0, 0).bitcast(BF16)
+        round_pair(rounded, w3_raw[1], low, negate_vector, "m j t")
+        quantize_pair(w3_mx[1], 0, rounded)
+        quantize_pair(w3_mx[0], 1, staged)
+        round_pair(rounded, w3_raw[1], high, negate_gpsimd, "m t j")
+        quantize_pair(w3_mx[1], 1, rounded)
+
+        slow_of(0, 0, product("c0_0", 4, c_late, 0, 0))
+        slow_of(1, 0, product("c1_0", 5, c_late, 1, 0))
+        nc.gpsimd.tensor_tensor(smooth[0][:, low, :], fresh_first, slow[0][:, low, :], ALU.add)
+        store_h(0, 0)
+        slow_of(0, 1, product("c0_1", 6, c_late, 0, 1))
+        nc.gpsimd.tensor_tensor(smooth_at(0, 1), fresh_second[:, 0, :], slow[1][:, 0, :], ALU.add)
+        for t, slot in ((2, 7), (3, 4)):
+            gated(slow[0][:, t, :], t, 0, product("e%d_0" % t, t - 1, b_terms + c_late, t, 0))
+            finish(t, 0, product("c%d_0" % t, slot, c_late, t, 0))
+        slow_of(1, 1, product("c1_1", 1, c_late, 1, 1))
+        nc.gpsimd.tensor_tensor(smooth_at(1, 1), fresh_second[:, 1, :], slow[1][:, 1, :], ALU.add)
+        store_h(1, 0)
+        root(0, slice(0, S))
+        square(0, slice(0, S))
+        root(1, slice(0, S))
+        square(1, cols(0))
+        weave(0, cast_scalar, 0, HALF)
+        store_h(0, 1)
+        gated(fresh_last[:], 2, 1, product("b2_1", 0, b_terms, 2, 1))
+        slow_of(2, 1, product("c2_1", 6, c_late, 2, 1))
+        gated(slow[1][:, 3, :], 3, 1, product("e3_1", 3, c_late + b_terms, 3, 1))
+        finish(3, 1, product("c3_1", 5, c_late, 3, 1))
+        nc.vector.tensor_tensor(smooth_at(2, 1), fresh_last[:], slow[1][:, 2, :], ALU.add)
+        store_h(1, 1)
         quantize_half(0)
-        for t in (2, 3):
-            nc.vector.tensor_tensor(smooth[1][:, t, :], late_fresh[:, t - 2, :], slow[1][:, t, :], ALU.add)
-            nc.sync.dma_start(h_view[:, t, cols1], smooth[1][:, t, :])
-        damping(1, 0, 2)
-        weave(1, 160)
-        damping(1, 2, 4)
-        damping(1, 4, 5)
-        damping(1, 5, 6)
-        for q in range(N_TILES):
-            adjust(0, q)
-            if q < 2:
-                store_y(0, q, q + 1)
-            elif q % 2:
-                store_y(0, q - 1, q + 1)
+        weave(1, cast_scalar, 0, SCALAR_WEAVE)
+        weave(1, cast_vector, SCALAR_WEAVE, HALF)
+        square(1, cols(1))
+        root(2, cols(0))
+        adjust(0, 0, 0)
         quantize_half(1)
         for q in range(QUADS):
             nc.sync.dma_start(
                 out_3[0, 4 * q : 4 * q + 4, :].bitcast(I32),
                 h_plane[32 * q + H_ROW : 32 * q + H_ROW + 4, :].bitcast(I32),
             )
+        freed = woven[1][:].bitcast(F32)
+        for q in range(2, N_TILES):
+            square_gpsimd(q, freed[:, cols(q - 2)] if q < 4 else None)
+            if q + 1 < N_TILES:
+                root(q + 1, cols(0))
+            root(q, cols(1))
+            square(q, cols(1))
         for q in range(N_TILES):
-            adjust(1, q)
-            if q in (1, 3):
-                store_y(1, q - 1, q + 1)
-            elif q > 3:
-                store_y(1, q, q + 1)
+            for h in range(HALVES):
+                if (q, h) != (0, 0):
+                    adjust(q, h, (2 * q + h) % 8)
+                if q == N_TILES - 1:
+                    nc.sync.dma_start(y_view[:, q, cols(h)], rows[q][:, cols(h)])
+            if q < N_TILES - 1:
+                nc.sync.dma_start(y_view[:, q, :], rows[q])

@@ -101,9 +101,9 @@ def tile_list_quote_smoothing_kernel(
         w1_raw = [load_weight("w1", w1, 0)]
         load_table(0, slice(0, T))
         move_scales(0)
-        load_table(1, slice(0, T // 2))
+        load_table(1, slice(0, 3 * T // 4))
         move_scales(1)
-        load_table(1, slice(T // 2, T))
+        load_table(1, slice(3 * T // 4, T))
         w1_raw.append(load_weight("w1", w1, 1))
         w3_raw = [load_weight("w3", w3, a) for a in range(PASSES)]
         inv_view = inv.rearrange("(q p) j -> p q j", p=P)
@@ -270,15 +270,18 @@ def tile_list_quote_smoothing_kernel(
             )
             nc.vector.tensor_tensor(rows[q][:, cols(h)], damp[q, h], acc[:], ALU.mult)
 
+        def negate_scalar(out, in_):
+            nc.scalar.activation(out, in_, ACT.Copy, scale=-1.0)
+
         def negate_vector(out, in_):
             nc.vector.tensor_scalar(out, in_, -1.0, None, ALU.mult)
 
         def negate_gpsimd(out, in_):
             nc.gpsimd.tensor_scalar(out, in_, -1.0, 0.0, ALU.mult, ALU.add)
 
-        def round_pair(grouped, raw, slots, cast, walk):
-            out = grouped.rearrange("p (t m j) -> p t m j", t=2, j=PACK)
-            source = raw[:].rearrange("p j (m t) -> p t m j", t=PACK)[:, slots]
+        def round_pair(grouped, raw, slots, cast, walk, columns=slice(0, P)):
+            out = grouped.rearrange("p (t m j) -> p t m j", t=2, j=PACK)[:, :, columns, :]
+            source = raw[:].rearrange("p j (m t) -> p t m j", t=PACK)[:, slots, columns, :]
             order = "p t m j -> p " + walk
             cast(out.rearrange(order), source.rearrange(order))
 
@@ -295,7 +298,7 @@ def tile_list_quote_smoothing_kernel(
 
         low, high = slice(0, 2), slice(2, 4)
         first_tiles = [(0, 0), (1, 0), (0, 1), (1, 1)]
-        second_tiles = [(3, 0), (2, 0), (3, 1), (2, 1)]
+        second_tiles = [(2, 0), (3, 0), (2, 1), (3, 1)]
 
         gather(0, 0)
         gather(0, 1)
@@ -329,50 +332,49 @@ def tile_list_quote_smoothing_kernel(
         staged = front[:, :HALF].bitcast(BF16)
         round_pair(early, w3_raw[0], low, negate_vector, "m j t")
         quantize_pair(w3_mx[0], 0, early)
-        round_pair(staged, w3_raw[0], high, negate_gpsimd, "m t j")
+        round_pair(staged, w3_raw[0], high, negate_gpsimd, "m t j", slice(0, P // 2))
+        round_pair(staged, w3_raw[0], high, negate_scalar, "m j t", slice(P // 2, P))
         gated(fresh_first[:, 0, :], 0, 0, acc_b[0, 0])
         gated(fresh_first[:, 1, :], 1, 0, acc_b[1, 0])
         gated(fresh_second[:, 0, :], 0, 1, acc_b[0, 1])
         gated(fresh_second[:, 1, :], 1, 1, acc_b[1, 1])
+        rounded = [sb("w3_bf1_0", [P, 2 * H], BF16)[:], smooth_at(0, 0).bitcast(BF16)]
+        round_pair(rounded[1], w3_raw[1], high, negate_scalar, "m j t")
         for n, (t, h) in enumerate(second_tiles):
             gate_of(t, h, product("a%d_%d" % (t, h), n, a_terms, t, h))
 
-        rounded = smooth_at(0, 0).bitcast(BF16)
-        round_pair(rounded, w3_raw[1], low, negate_vector, "m j t")
-        quantize_pair(w3_mx[1], 0, rounded)
+        round_pair(rounded[0], w3_raw[1], low, negate_vector, "m j t")
+        quantize_pair(w3_mx[1], 0, rounded[0])
         quantize_pair(w3_mx[0], 1, staged)
-        round_pair(rounded, w3_raw[1], high, negate_gpsimd, "m t j")
-        quantize_pair(w3_mx[1], 1, rounded)
+        quantize_pair(w3_mx[1], 1, rounded[1])
 
-        slow_of(0, 0, product("c0_0", 4, c_late, 0, 0))
-        slow_of(1, 0, product("c1_0", 5, c_late, 1, 0))
+        slow_of(0, 0, product("c0_0", 4, c_terms, 0, 0))
+        slow_of(1, 0, product("c1_0", 5, c_terms, 1, 0))
         nc.gpsimd.tensor_tensor(smooth[0][:, low, :], fresh_first, slow[0][:, low, :], ALU.add)
         store_h(0, 0)
-        slow_of(0, 1, product("c0_1", 6, c_late, 0, 1))
+        slow_of(0, 1, product("c0_1", 6, c_terms, 0, 1))
         nc.gpsimd.tensor_tensor(smooth_at(0, 1), fresh_second[:, 0, :], slow[1][:, 0, :], ALU.add)
         for t, slot in ((2, 7), (3, 4)):
-            gated(slow[0][:, t, :], t, 0, product("e%d_0" % t, t - 1, b_terms + c_late, t, 0))
-            finish(t, 0, product("c%d_0" % t, slot, c_late, t, 0))
-        slow_of(1, 1, product("c1_1", 1, c_late, 1, 1))
+            gated(slow[0][:, t, :], t, 0, product("e%d_0" % t, t - 2, b_terms + c_late, t, 0))
+            finish(t, 0, product("c%d_0" % t, slot, c_terms, t, 0))
+        slow_of(1, 1, product("c1_1", 0, c_terms, 1, 1))
         nc.gpsimd.tensor_tensor(smooth_at(1, 1), fresh_second[:, 1, :], slow[1][:, 1, :], ALU.add)
         store_h(1, 0)
-        root(0, slice(0, S))
-        square(0, slice(0, S))
-        root(1, slice(0, S))
-        square(1, cols(0))
+        root(0, cols(0))
+        square(0, cols(0))
         weave(0, cast_scalar, 0, HALF)
         store_h(0, 1)
-        gated(fresh_last[:], 2, 1, product("b2_1", 0, b_terms, 2, 1))
-        slow_of(2, 1, product("c2_1", 6, c_late, 2, 1))
+        gated(fresh_last[:], 2, 1, product("b2_1", 2, b_terms, 2, 1))
+        slow_of(2, 1, product("c2_1", 6, c_terms, 2, 1))
         gated(slow[1][:, 3, :], 3, 1, product("e3_1", 3, c_late + b_terms, 3, 1))
-        finish(3, 1, product("c3_1", 5, c_late, 3, 1))
+        finish(3, 1, product("c3_1", 5, c_terms, 3, 1))
         nc.vector.tensor_tensor(smooth_at(2, 1), fresh_last[:], slow[1][:, 2, :], ALU.add)
         store_h(1, 1)
         quantize_half(0)
         weave(1, cast_scalar, 0, SCALAR_WEAVE)
         weave(1, cast_vector, SCALAR_WEAVE, HALF)
-        square(1, cols(1))
-        root(2, cols(0))
+        root(0, cols(1))
+        square(0, cols(1))
         adjust(0, 0, 0)
         quantize_half(1)
         for q in range(QUADS):
@@ -380,6 +382,11 @@ def tile_list_quote_smoothing_kernel(
                 out_3[0, 4 * q : 4 * q + 4, :].bitcast(I32),
                 h_plane[32 * q + H_ROW : 32 * q + H_ROW + 4, :].bitcast(I32),
             )
+        root(1, cols(0))
+        root(2, cols(0))
+        square(1, cols(0))
+        root(1, cols(1))
+        square(1, cols(1))
         freed = woven[1][:].bitcast(F32)
         for q in range(2, N_TILES):
             square_gpsimd(q, freed[:, cols(q - 2)] if q < 4 else None)

@@ -26,7 +26,6 @@ HALVES = S // HALF
 N_TILES = N // P
 W4_ROW = 4
 H_ROW = 12
-SCALAR_WEAVE = 256
 
 
 def tile_list_quote_smoothing_kernel(
@@ -371,8 +370,7 @@ def tile_list_quote_smoothing_kernel(
         nc.vector.tensor_tensor(smooth_at(2, 1), fresh_last[:], slow[1][:, 2, :], ALU.add)
         store_h(1, 1)
         quantize_half(0)
-        weave(1, cast_scalar, 0, SCALAR_WEAVE)
-        weave(1, cast_vector, SCALAR_WEAVE, HALF)
+        weave(1, cast_vector, 0, HALF)
         root(0, cols(1))
         square(0, cols(1))
         adjust(0, 0, 0)

@@ -100,9 +100,8 @@ def tile_list_quote_smoothing_kernel(
         w1_raw = [load_weight("w1", w1, 0)]
         load_table(0, slice(0, T))
         move_scales(0)
-        load_table(1, slice(0, 3 * T // 4))
+        load_table(1, slice(0, T))
         move_scales(1)
-        load_table(1, slice(3 * T // 4, T))
         w1_raw.append(load_weight("w1", w1, 1))
         w3_raw = [load_weight("w3", w3, a) for a in range(PASSES)]
         inv_view = inv.rearrange("(q p) j -> p q j", p=P)
@@ -118,13 +117,13 @@ def tile_list_quote_smoothing_kernel(
         load_inv(1, 2)
         w4_codes = sb("w4_codes", [P, N], I32)
         nc.sync.dma_start(w4_codes[:], w4_words[0].rearrange("p n i -> p (n i)").bitcast(I32))
+        load_inv(2, 4)
+        load_inv(4, 6)
         for q in range(QUADS):
             nc.sync.dma_start(
                 w4_plane[32 * q + W4_ROW : 32 * q + W4_ROW + 4, :].bitcast(I32),
                 w4_scales[0, 4 * q : 4 * q + 4, :].bitcast(I32),
             )
-        load_inv(2, 4)
-        load_inv(4, 6)
 
         def cast_scalar(out, in_):
             nc.scalar.activation(out, in_, ACT.Copy)
@@ -375,11 +374,6 @@ def tile_list_quote_smoothing_kernel(
         square(0, cols(1))
         adjust(0, 0, 0)
         quantize_half(1)
-        for q in range(QUADS):
-            nc.sync.dma_start(
-                out_3[0, 4 * q : 4 * q + 4, :].bitcast(I32),
-                h_plane[32 * q + H_ROW : 32 * q + H_ROW + 4, :].bitcast(I32),
-            )
         root(1, cols(0))
         root(2, cols(0))
         square(1, cols(0))
@@ -392,11 +386,18 @@ def tile_list_quote_smoothing_kernel(
                 root(q + 1, cols(0))
             root(q, cols(1))
             square(q, cols(1))
+        turn = 1
         for q in range(N_TILES):
-            for h in range(HALVES):
+            for h in (1, 0):
                 if (q, h) != (0, 0):
-                    adjust(q, h, (2 * q + h) % 8)
+                    adjust(q, h, turn % 4)
+                    turn = turn + 1
                 if q == N_TILES - 1:
                     nc.sync.dma_start(y_view[:, q, cols(h)], rows[q][:, cols(h)])
             if q < N_TILES - 1:
                 nc.sync.dma_start(y_view[:, q, :], rows[q])
+        for q in range(QUADS):
+            nc.scalar.dma_start(
+                out_3[0, 4 * q : 4 * q + 4, :].bitcast(I32),
+                h_plane[32 * q + H_ROW : 32 * q + H_ROW + 4, :].bitcast(I32),
+            )

@@ -64,8 +64,8 @@ def tile_list_quote_smoothing_kernel(
         )
         for q in range(QUADS):
             nc.scalar.dma_start(
-                w2_rows[32 * q : 32 * q + 4, :].bitcast(I32).rearrange("r (a e) -> r a e", a=PASSES),
-                w2_scales[:, 4 * q : 4 * q + 4, :].bitcast(I32).rearrange("a r e -> r a e"),
+                w2_rows[q:P:32, :].bitcast(I32).rearrange("r (a e) -> r a e", a=PASSES),
+                w2_scales[:, q:16:4, :].bitcast(I32).rearrange("a r e -> r a e"),
             )
 
         def load_weight(name, w, a):
@@ -91,10 +91,9 @@ def tile_list_quote_smoothing_kernel(
 
         def move_scales(a):
             for q in range(QUADS):
-                row = 16 * a + 4 * q
                 nc.sync.dma_start(
-                    v_plane[a][32 * q : 32 * q + 4, :].bitcast(I32),
-                    picked_rows[row : row + 4, :].bitcast(I32),
+                    v_plane[a][q:P:32, :].bitcast(I32),
+                    picked_rows[16 * a + q : 16 * (a + 1) : 4, :].bitcast(I32),
                 )
 
         w1_raw = [load_weight("w1", w1, 0)]
@@ -121,8 +120,8 @@ def tile_list_quote_smoothing_kernel(
         load_inv(4, 6)
         for q in range(QUADS):
             nc.sync.dma_start(
-                w4_plane[32 * q + W4_ROW : 32 * q + W4_ROW + 4, :].bitcast(I32),
-                w4_scales[0, 4 * q : 4 * q + 4, :].bitcast(I32),
+                w4_plane[W4_ROW + q : P : 32, :].bitcast(I32),
+                w4_scales[0, q:16:4, :].bitcast(I32),
             )
 
         def cast_scalar(out, in_):
@@ -398,6 +397,6 @@ def tile_list_quote_smoothing_kernel(
                 nc.sync.dma_start(y_view[:, q, :], rows[q])
         for q in range(QUADS):
             nc.scalar.dma_start(
-                out_3[0, 4 * q : 4 * q + 4, :].bitcast(I32),
-                h_plane[32 * q + H_ROW : 32 * q + H_ROW + 4, :].bitcast(I32),
+                out_3[0, q:16:4, :].bitcast(I32),
+                h_plane[H_ROW + q : P : 32, :].bitcast(I32),
             )

@@ -26,6 +26,7 @@ HALVES = S // HALF
 N_TILES = N // P
 W4_ROW = 4
 H_ROW = 12
+VECTOR_COLUMNS = 88
 
 
 def tile_list_quote_smoothing_kernel(
@@ -311,7 +312,8 @@ def tile_list_quote_smoothing_kernel(
 
         w1_mx.append((sb("w1_1_codes", [P, H], U32), sb("w1_1_plane", [P, H], U8)))
         late = [sb("w1_bf1_%d" % u, [P, 2 * H], BF16) for u in range(2)]
-        round_pair(late[0][:], w1_raw[1], low, cast_vector, "m j t")
+        round_pair(late[0][:], w1_raw[1], low, cast_vector, "m j t", slice(0, VECTOR_COLUMNS))
+        round_pair(late[0][:], w1_raw[1], low, cast_scalar, "m j t", slice(VECTOR_COLUMNS, P))
         round_pair(late[1][:], w1_raw[1], high, cast_scalar, "m j t")
         for u in range(2):
             quantize_pair(w1_mx[1], u, late[u][:])
@@ -346,8 +348,9 @@ def tile_list_quote_smoothing_kernel(
         quantize_pair(w3_mx[1], 1, rounded[1])
 
         slow_of(0, 0, product("c0_0", 4, c_terms, 0, 0))
+        nc.gpsimd.tensor_tensor(smooth_at(0, 0), fresh_first[:, 0, :], slow[0][:, 0, :], ALU.add)
         slow_of(1, 0, product("c1_0", 5, c_terms, 1, 0))
-        nc.gpsimd.tensor_tensor(smooth[0][:, low, :], fresh_first, slow[0][:, low, :], ALU.add)
+        nc.gpsimd.tensor_tensor(smooth_at(1, 0), fresh_first[:, 1, :], slow[0][:, 1, :], ALU.add)
         store_h(0, 0)
         slow_of(0, 1, product("c0_1", 6, c_terms, 0, 1))
         nc.gpsimd.tensor_tensor(smooth_at(0, 1), fresh_second[:, 0, :], slow[1][:, 0, :], ALU.add)
@@ -380,11 +383,16 @@ def tile_list_quote_smoothing_kernel(
         square(1, cols(1))
         freed = woven[1][:].bitcast(F32)
         for q in range(2, N_TILES):
-            square_gpsimd(q, freed[:, cols(q - 2)] if q < 4 else None)
-            if q + 1 < N_TILES:
+            if q == 4:
+                square(q, cols(0))
+            else:
+                square_gpsimd(q, freed[:, cols(q - 2)] if q < 4 else None)
+            if q < 4:
                 root(q + 1, cols(0))
             root(q, cols(1))
             square(q, cols(1))
+            if q == 4:
+                root(q + 1, cols(0))
         turn = 1
         for q in range(N_TILES):
             for h in (1, 0):

@@ -118,12 +118,12 @@ def tile_list_quote_smoothing_kernel(
         w4_codes = sb("w4_codes", [P, N], I32)
         nc.sync.dma_start(w4_codes[:], w4_words[0].rearrange("p n i -> p (n i)").bitcast(I32))
         load_inv(2, 4)
-        load_inv(4, 6)
         for q in range(QUADS):
             nc.sync.dma_start(
                 w4_plane[W4_ROW + q : P : 32, :].bitcast(I32),
                 w4_scales[0, q:16:4, :].bitcast(I32),
             )
+        load_inv(4, 6)
 
         def cast_scalar(out, in_):
             nc.scalar.activation(out, in_, ACT.Copy)
@@ -375,6 +375,7 @@ def tile_list_quote_smoothing_kernel(
         root(0, cols(1))
         square(0, cols(1))
         adjust(0, 0, 0)
+        nc.sync.dma_start(y_view[:, 0, cols(0)], rows[0][:, cols(0)])
         quantize_half(1)
         root(1, cols(0))
         root(2, cols(0))
@@ -382,26 +383,25 @@ def tile_list_quote_smoothing_kernel(
         root(1, cols(1))
         square(1, cols(1))
         freed = woven[1][:].bitcast(F32)
-        for q in range(2, N_TILES):
-            if q == 4:
-                square(q, cols(0))
-            else:
-                square_gpsimd(q, freed[:, cols(q - 2)] if q < 4 else None)
-            if q < 4:
-                root(q + 1, cols(0))
+        spare = [freed[:, cols(0)], freed[:, cols(1)], None]
+        for q in range(2, N_TILES - 1):
+            square_gpsimd(q, spare[q - 2])
             root(q, cols(1))
+            root(q + 1, cols(0))
             square(q, cols(1))
-            if q == 4:
-                root(q + 1, cols(0))
+        square(N_TILES - 1, cols(0))
+        root(N_TILES - 1, cols(1))
+        square(N_TILES - 1, cols(1))
         turn = 1
         for q in range(N_TILES):
-            for h in (1, 0):
+            in_halves = q in (0, N_TILES - 1)
+            for h in (1, 0) if q < N_TILES - 1 else (0, 1):
                 if (q, h) != (0, 0):
                     adjust(q, h, turn % 4)
                     turn = turn + 1
-                if q == N_TILES - 1:
-                    nc.sync.dma_start(y_view[:, q, cols(h)], rows[q][:, cols(h)])
-            if q < N_TILES - 1:
+                    if in_halves:
+                        nc.sync.dma_start(y_view[:, q, cols(h)], rows[q][:, cols(h)])
+            if not in_halves:
                 nc.sync.dma_start(y_view[:, q, :], rows[q])
         for q in range(QUADS):
             nc.scalar.dma_start(

from contextlib import ExitStack

import concourse.mybir as mybir

K, T, S, H, N = 1024, 4096, 1024, 512, 768
FLOPS = 2 * S * (3 * K * H + H * N)

F32 = mybir.dt.float32
BF16 = mybir.dt.bfloat16
I32 = mybir.dt.int32
U32 = mybir.dt.uint32
U16 = mybir.dt.uint16
U8 = mybir.dt.uint8
FP8X4 = mybir.dt.float8_e4m3fn_x4
FP4X4 = mybir.dt.float4_e2m1fn_x4
ACT = mybir.ActivationFunctionType
ALU = mybir.AluOpType

P = 128
PACK = 4
K_PASS = P * PACK
PASSES = K // K_PASS
QUADS = 4
HALF = 512
HALVES = S // HALF
N_TILES = N // P
W4_ROW = 4
H_ROW = 12
VECTOR_COLUMNS = 88


def tile_list_quote_smoothing_kernel(
    tc, tab_words, tab_scales, offs, w1, w2_words, w2_scales, w3, w4_words, w4_scales, inv,
    out_0, out_1, out_2, out_3,
):
    nc = tc.nc
    with ExitStack() as ctx:
        lists = ctx.enter_context(tc.tile_pool(name="lists", bufs=1))
        keep = ctx.enter_context(tc.tile_pool(name="keep", bufs=1))
        psum = ctx.enter_context(tc.psum_pool(name="psum", bufs=1))

        def sb(name, shape, dtype):
            return keep.tile(shape, dtype, name=name, align_bytes=64)

        offsets = lists.tile([P, S // 16], U16, name="offsets")
        tab_rows = sb("tab_rows", [P, T], U8)
        w2_rows = sb("w2_rows", [P, PASSES * H], U8)
        w4_plane = sb("w4_plane", [P, N], U8)
        v_plane = [sb("v_plane%d" % a, [P, S], U8) for a in range(PASSES)]
        one = sb("one", [P, 1], F32)

        nc.vector.memset(w2_rows[:].bitcast(I32), 0)
        nc.vector.memset(one[:], 1.0)
        nc.vector.memset(tab_rows[32:64, :].bitcast(I32), 0)
        nc.vector.memset(tab_rows[64:128, :].bitcast(I32), 0)
        for a in range(PASSES):
            nc.vector.memset(v_plane[a][:].bitcast(I32), 0)
        nc.vector.memset(w4_plane[:].bitcast(I32), 0)

        warm = sb("warm", [P, 1], F32)
        nc.scalar.activation(warm[:], one[:], ACT.Sigmoid)
        nc.sync.dma_start(offsets[:], offs)
        nc.sync.dma_start(
            tab_rows[0:32, :].bitcast(I32), tab_scales.rearrange("a q t -> (a q) t").bitcast(I32)
        )
        for q in range(QUADS):
            nc.scalar.dma_start(
                w2_rows[q:P:32, :].bitcast(I32).rearrange("r (a e) -> r a e", a=PASSES),
                w2_scales[:, q:16:4, :].bitcast(I32).rearrange("a r e -> r a e"),
            )

        def load_weight(name, w, a):
            raw = sb("%s_raw%d" % (name, a), [P, PACK, H], F32)
            nc.sync.dma_start(
                raw[:], w[a * K_PASS : (a + 1) * K_PASS, :].rearrange("(p j) c -> p j c", j=PACK)
            )
            return raw

        w2_raw = sb("w2_raw", [P, PASSES * 2 * H], U8)
        nc.sync.dma_start(
            w2_raw[:].bitcast(I32).rearrange("p (a e) -> p a e", a=PASSES),
            w2_words.bitcast(I32).rearrange("a p e -> p a e"),
        )
        picked_rows = sb("picked_rows", [P, S], U8)
        nc.vector.tensor_copy(picked_rows[:], tab_rows[:].indirect(offsets[:]))

        table = [sb("table%d" % a, [P, T], I32) for a in range(PASSES)]

        def load_table(a, cols):
            words = tab_words[a].rearrange("p n i -> p (n i)").bitcast(I32)
            nc.sync.dma_start(table[a][:, cols], words[:, cols])

        def move_scales(a):
            for q in range(QUADS):
                nc.sync.dma_start(
                    v_plane[a][q:P:32, :].bitcast(I32),
                    picked_rows[16 * a + q : 16 * (a + 1) : 4, :].bitcast(I32),
                )

        w1_raw = [load_weight("w1", w1, 0)]
        load_table(0, slice(0, T))
        move_scales(0)
        load_table(1, slice(0, T))
        move_scales(1)
        w1_raw.append(load_weight("w1", w1, 1))
        w3_raw = [load_weight("w3", w3, a) for a in range(PASSES)]
        inv_view = inv.rearrange("(q p) j -> p q j", p=P)
        rows = {}

        def load_inv(q0, q1):
            tile = sb("inv%d" % q0, [P, q1 - q0, S], F32)
            nc.sync.dma_start(tile[:], inv_view[:, q0:q1, :])
            for q in range(q0, q1):
                rows[q] = tile[:, q - q0, :]

        load_inv(0, 1)
        load_inv(1, 2)
        w4_codes = sb("w4_codes", [P, N], I32)
        nc.sync.dma_start(w4_codes[:], w4_words[0].rearrange("p n i -> p (n i)").bitcast(I32))
        load_inv(2, 4)
        for q in range(QUADS):
            nc.sync.dma_start(
                w4_plane[W4_ROW + q : P : 32, :].bitcast(I32),
                w4_scales[0, q:16:4, :].bitcast(I32),
            )
        load_inv(4, 6)

        def cast_scalar(out, in_):
            nc.scalar.activation(out, in_, ACT.Copy)

        def cast_gpsimd(out, in_):
            nc.gpsimd.tensor_copy(out, in_)

        def cast_vector(out, in_):
            nc.vector.tensor_copy(out, in_)

        def round_weight(name, raw, cast, walk):
            grouped = sb(name, [P, PACK * H], BF16)
            cast(
                grouped[:].rearrange("p (t m j) -> p " + walk, t=PACK, j=PACK),
                raw[:].rearrange("p j (m t) -> p " + walk, t=PACK),
            )
            return grouped

        def quantize_weight(name, grouped):
            codes = sb(name + "_codes", [P, H], U32)
            plane = sb(name + "_plane", [P, H], U8)
            nc.vector.quantize_mx(out=codes[:].bitcast(FP8X4), scales=plane[:], in_=grouped[:])
            return codes, plane

        w1_bf = round_weight("w1_bf0", w1_raw[0], cast_scalar, "m j t")

        w2_codes = sb("w2_codes", [P, PASSES * 2 * H], U8)
        nc.vector.tensor_copy(
            w2_codes[:].rearrange("p (a t m b) -> p a t m b", a=PASSES, t=PACK, b=2),
            w2_raw[:].rearrange("p (a m t b) -> p a t m b", a=PASSES, t=PACK, b=2),
        )
        w2_plane = sb("w2_plane", [P, PASSES * H], U8)
        nc.vector.tensor_copy(
            w2_plane[:].rearrange("p (a t m) -> p a t m", a=PASSES, t=PACK),
            w2_rows[:].rearrange("p (a m t) -> p a t m", a=PASSES, t=PACK),
        )
        w1_mx = [quantize_weight("w1_0", w1_bf)]

        v_codes = {}

        def gather(a, h):
            tile = sb("v_codes%d_%d" % (a, h), [P, HALF], U32)
            cols = HALF // 16
            nc.vector.tensor_copy(
                tile[:], table[a][:].bitcast(U32).indirect(offsets[:, h * cols : (h + 1) * cols])
            )
            v_codes[a, h] = tile

        def fp8_operand(mx):
            def pick(a, t):
                codes, plane = mx[a]
                return codes[:, t * P : (t + 1) * P].bitcast(FP8X4), plane[:, t * P : (t + 1) * P]
            return pick

        def w2_operand(a, t):
            col = a * H + t * P
            return w2_codes[:, 2 * col : 2 * (col + P)].bitcast(FP4X4), w2_plane[:, col : col + P]

        def bank(name, slot):
            return psum.tile([P, HALF], F32, name=name, tag="bank%d" % slot)

        def mx_pass(acc, operand, a, t, h, first=None, final=None):
            codes, plane = operand(a, t)
            nc.tensor.matmul_mx(
                out=acc[:], lhsT=codes, lhsT_scale=plane,
                rhs=v_codes[a, h][:].bitcast(FP8X4),
                rhs_scale=v_plane[a][:, h * HALF : (h + 1) * HALF],
                start=(a == 0) if first is None else first,
                stop=(a == PASSES - 1) if final is None else final,
            )

        w1_operand = fp8_operand(w1_mx)
        gate = {(t, h): sb("gate%d_%d" % (t, h), [P, HALF], F32) for t in range(PACK) for h in range(HALVES)}
        smooth = [sb("smooth%d" % h, [P, PACK, HALF], F32)[:] for h in range(HALVES)]
        fresh_second = sb("fresh_second", [P, 2, HALF], F32)
        front = sb("front", [P, 3 * HALF], F32)
        fresh_first = front[:, HALF:].rearrange("p (t j) -> p t j", t=2)
        fresh_last = sb("fresh_last", [P, HALF], F32)
        slow = [sb("slow%d" % h, [P, PACK, HALF], F32) for h in range(HALVES)]

        def cols(h):
            return slice(h * HALF, (h + 1) * HALF)

        def smooth_at(t, h):
            return smooth[h][:, t, :]

        h_codes = sb("h_codes", [P, S], U32)
        h_plane = sb("h_plane", [P, S], U8)
        h_view = out_1.rearrange("(p t) j -> p t j", t=PACK)
        words_view = out_2[0].rearrange("p m i -> p (m i)").bitcast(I32)
        y_view = out_0.rearrange("(q p) j -> p q j", p=P)
        woven = [sb("woven%d" % h, [P, PACK * HALF], BF16) for h in range(HALVES)]

        def gate_of(t, h, acc):
            nc.scalar.activation(gate[t, h][:], acc[:], ACT.Sigmoid)

        def gated(out, t, h, acc):
            nc.vector.tensor_tensor(out, gate[t, h][:], acc[:], ALU.mult)

        def slow_of(t, h, minus_c):
            nc.vector.scalar_tensor_tensor(slow[h][:, t, :], gate[t, h][:], 1.0, minus_c[:], ALU.subtract, ALU.mult)

        def finish(t, h, minus_c):
            nc.vector.tensor_tensor(smooth_at(t, h), slow[h][:, t, :], minus_c[:], ALU.subtract)

        def store_h(u, h):
            pair = slice(2 * u, 2 * u + 2)
            nc.sync.dma_start(h_view[:, pair, cols(h)], smooth[h][:, pair, :])

        def weave(h, cast, c0, c1):
            cast(
                woven[h][:, PACK * c0 : PACK * c1].rearrange("p (c i t) -> p c t i", i=4, t=PACK),
                smooth[h][:, :, c0:c1].rearrange("p t (c i) -> p c t i", i=4),
            )

        def quantize_half(h):
            nc.vector.quantize_mx(out=h_codes[:, cols(h)].bitcast(FP8X4), scales=h_plane[H_ROW:, cols(h)], in_=woven[h][:])
            nc.sync.dma_start(words_view[:, cols(h)], h_codes[:, cols(h)].bitcast(I32))

        def root(q, span):
            nc.scalar.activation(rows[q][:, span], rows[q][:, span], ACT.Abs_reciprocal_sqrt, bias=one[:])

        def square(q, span):
            nc.scalar.activation(rows[q][:, span], rows[q][:, span], ACT.Square)

        damp = {(q, h): rows[q][:, cols(h)] for q in range(N_TILES) for h in range(HALVES)}

        def square_gpsimd(q, out=None):
            source = rows[q][:, cols(0)]
            if out is not None:
                damp[q, 0] = out
            nc.gpsimd.tensor_tensor(damp[q, 0], source, source, ALU.mult)

        def adjust(q, h, slot):
            n0 = q * P
            acc = bank("d%d_%d" % (q, h), slot)
            nc.tensor.matmul_mx(
                out=acc[:], lhsT=w4_codes[:, n0 : n0 + P].bitcast(FP8X4),
                lhsT_scale=w4_plane[W4_ROW:, n0 : n0 + P],
                rhs=h_codes[:, cols(h)].bitcast(FP8X4), rhs_scale=h_plane[H_ROW:, cols(h)],
                start=True, stop=True,
            )
            nc.vector.tensor_tensor(rows[q][:, cols(h)], damp[q, h], acc[:], ALU.mult)

        def negate_scalar(out, in_):
            nc.scalar.activation(out, in_, ACT.Copy, scale=-1.0)

        def negate_vector(out, in_):
            nc.vector.tensor_scalar(out, in_, -1.0, None, ALU.mult)

        def negate_gpsimd(out, in_):
            nc.gpsimd.tensor_scalar(out, in_, -1.0, 0.0, ALU.mult, ALU.add)

        def round_pair(grouped, raw, slots, cast, walk, columns=slice(0, P)):
            out = grouped.rearrange("p (t m j) -> p t m j", t=2, j=PACK)[:, :, columns, :]
            source = raw[:].rearrange("p j (m t) -> p t m j", t=PACK)[:, slots, columns, :]
            order = "p t m j -> p " + walk
            cast(out.rearrange(order), source.rearrange(order))

        def quantize_pair(mx, u, grouped):
            codes, plane = mx
            span = slice(2 * u * P, 2 * (u + 1) * P)
            nc.vector.quantize_mx(out=codes[:, span].bitcast(FP8X4), scales=plane[:, span], in_=grouped)

        def product(name, slot, terms, t, h):
            acc = bank(name, slot)
            for n, (operand, a) in enumerate(terms):
                mx_pass(acc, operand, a, t, h, first=(n == 0), final=(n == len(terms) - 1))
            return acc

        low, high = slice(0, 2), slice(2, 4)
        first_tiles = [(0, 0), (1, 0), (0, 1), (1, 1)]
        second_tiles = [(2, 0), (3, 0), (2, 1), (3, 1)]

        gather(0, 0)
        gather(0, 1)
        acc_a = {tile: bank("a%d_%d" % tile, n) for n, tile in enumerate(first_tiles)}
        acc_b = {tile: bank("b%d_%d" % tile, PACK + n) for n, tile in enumerate(first_tiles)}
        for t, h in first_tiles:
            mx_pass(acc_a[t, h], w1_operand, 0, t, h)
            mx_pass(acc_b[t, h], w2_operand, 0, t, h)
        gather(1, 0)
        gather(1, 1)
        for t, h in first_tiles:
            mx_pass(acc_b[t, h], w2_operand, 1, t, h)

        w1_mx.append((sb("w1_1_codes", [P, H], U32), sb("w1_1_plane", [P, H], U8)))
        late = [sb("w1_bf1_%d" % u, [P, 2 * H], BF16) for u in range(2)]
        round_pair(late[0][:], w1_raw[1], low, cast_vector, "m j t", slice(0, VECTOR_COLUMNS))
        round_pair(late[0][:], w1_raw[1], low, cast_scalar, "m j t", slice(VECTOR_COLUMNS, P))
        round_pair(late[1][:], w1_raw[1], high, cast_scalar, "m j t")
        for u in range(2):
            quantize_pair(w1_mx[1], u, late[u][:])
        for t, h in first_tiles:
            mx_pass(acc_a[t, h], w1_operand, 1, t, h)
        a_terms = [(w1_operand, a) for a in range(PASSES)]
        b_terms = [(w2_operand, a) for a in range(PASSES)]
        for t, h in first_tiles:
            gate_of(t, h, acc_a[t, h])
        w3_mx = [(sb("w3_%d_codes" % a, [P, H], U32), sb("w3_%d_plane" % a, [P, H], U8)) for a in range(PASSES)]
        w3_operand = fp8_operand(w3_mx)
        c_terms = [(w3_operand, a) for a in range(PASSES)]
        c_late = c_terms[::-1]
        early = front[:, HALF // 2 : 3 * HALF // 2].bitcast(BF16)
        staged = front[:, :HALF].bitcast(BF16)
        round_pair(early, w3_raw[0], low, negate_vector, "m j t")
        quantize_pair(w3_mx[0], 0, early)
        round_pair(staged, w3_raw[0], high, negate_gpsimd, "m t j", slice(0, P // 2))
        round_pair(staged, w3_raw[0], high, negate_scalar, "m j t", slice(P // 2, P))
        gated(fresh_first[:, 0, :], 0, 0, acc_b[0, 0])
        gated(fresh_first[:, 1, :], 1, 0, acc_b[1, 0])
        gated(fresh_second[:, 0, :], 0, 1, acc_b[0, 1])
        gated(fresh_second[:, 1, :], 1, 1, acc_b[1, 1])
        rounded = [sb("w3_bf1_0", [P, 2 * H], BF16)[:], smooth_at(0, 0).bitcast(BF16)]
        round_pair(rounded[1], w3_raw[1], high, negate_scalar, "m j t")
        for n, (t, h) in enumerate(second_tiles):
            gate_of(t, h, product("a%d_%d" % (t, h), n, a_terms, t, h))

        round_pair(rounded[0], w3_raw[1], low, negate_vector, "m j t")
        quantize_pair(w3_mx[1], 0, rounded[0])
        quantize_pair(w3_mx[0], 1, staged)
        quantize_pair(w3_mx[1], 1, rounded[1])

        slow_of(0, 0, product("c0_0", 4, c_terms, 0, 0))
        nc.gpsimd.tensor_tensor(smooth_at(0, 0), fresh_first[:, 0, :], slow[0][:, 0, :], ALU.add)
        slow_of(1, 0, product("c1_0", 5, c_terms, 1, 0))
        nc.gpsimd.tensor_tensor(smooth_at(1, 0), fresh_first[:, 1, :], slow[0][:, 1, :], ALU.add)
        store_h(0, 0)
        slow_of(0, 1, product("c0_1", 6, c_terms, 0, 1))
        nc.gpsimd.tensor_tensor(smooth_at(0, 1), fresh_second[:, 0, :], slow[1][:, 0, :], ALU.add)
        for t, slot in ((2, 7), (3, 4)):
            gated(slow[0][:, t, :], t, 0, product("e%d_0" % t, t - 2, b_terms + c_late, t, 0))
            finish(t, 0, product("c%d_0" % t, slot, c_terms, t, 0))
        slow_of(1, 1, product("c1_1", 0, c_terms, 1, 1))
        nc.gpsimd.tensor_tensor(smooth_at(1, 1), fresh_second[:, 1, :], slow[1][:, 1, :], ALU.add)
        store_h(1, 0)
        root(0, cols(0))
        square(0, cols(0))
        weave(0, cast_scalar, 0, HALF)
        store_h(0, 1)
        gated(fresh_last[:], 2, 1, product("b2_1", 2, b_terms, 2, 1))
        slow_of(2, 1, product("c2_1", 6, c_terms, 2, 1))
        gated(slow[1][:, 3, :], 3, 1, product("e3_1", 3, c_late + b_terms, 3, 1))
        finish(3, 1, product("c3_1", 5, c_terms, 3, 1))
        nc.vector.tensor_tensor(smooth_at(2, 1), fresh_last[:], slow[1][:, 2, :], ALU.add)
        store_h(1, 1)
        quantize_half(0)
        weave(1, cast_vector, 0, HALF)
        root(0, cols(1))
        square(0, cols(1))
        adjust(0, 0, 0)
        nc.sync.dma_start(y_view[:, 0, cols(0)], rows[0][:, cols(0)])
        quantize_half(1)
        root(1, cols(0))
        root(2, cols(0))
        square(1, cols(0))
        root(1, cols(1))
        square(1, cols(1))
        freed = woven[1][:].bitcast(F32)
        spare = [freed[:, cols(0)], freed[:, cols(1)], None]
        for q in range(2, N_TILES - 1):
            square_gpsimd(q, spare[q - 2])
            root(q, cols(1))
            root(q + 1, cols(0))
            square(q, cols(1))
        square(N_TILES - 1, cols(0))
        root(N_TILES - 1, cols(1))
        square(N_TILES - 1, cols(1))
        turn = 1
        for q in range(N_TILES):
            in_halves = q in (0, N_TILES - 1)
            for h in (1, 0) if q < N_TILES - 1 else (0, 1):
                if (q, h) != (0, 0):
                    adjust(q, h, turn % 4)
                    turn = turn + 1
                    if in_halves:
                        nc.sync.dma_start(y_view[:, q, cols(h)], rows[q][:, cols(h)])
            if not in_halves:
                nc.sync.dma_start(y_view[:, q, :], rows[q])
        for q in range(QUADS):
            nc.scalar.dma_start(
                out_3[0, q:16:4, :].bitcast(I32),
                h_plane[H_ROW + q : P : 32, :].bitcast(I32),
            )
